import numpy as np, ml_dtypes
CORES = [1,5,17,21,33,37,49,53]
N = 8
import mx_ref
BF = ml_dtypes.bfloat16
def pick(q, e):
    c = np.concatenate([q[0].reshape(128, -1, 4), np.zeros((128, 1, 4), np.uint8)], axis=1); s = np.concatenate([q[1], np.ones((16, 1), np.uint8)], axis=1)
    return (np.ascontiguousarray(c[:, e].reshape(128, -1)), np.ascontiguousarray(s[:, e]))
def join(*qs):
    return (np.concatenate([q[0] for q in qs], axis=1), np.concatenate([q[1] for q in qs], axis=1))
def put(q, e, v):
    c, s = q[0].reshape(128, -1, 4).copy(), q[1].copy(); c[:, e] = v[0].reshape(128, -1, 4); s[:, e] = v[1]
    return (c.reshape(128, -1), s)
def pk(c, s):
    return (np.ascontiguousarray(c), mx_ref.live(s))
def emit(q):
    return q[0], q[1]
def tile(rs):
    return np.stack(rs, axis=2).reshape(128, -1).astype(BF)
def cut(t, i, w=512):
    return t[:, w * i:w * i + w]
def f(rng, *shape):
    return mx_ref.flush((rng.standard_normal(shape, dtype=np.float32) * np.exp2(rng.integers(-2, 3, shape[:-1] + (1,)))).astype(BF))
def wide(rng, *shape, cols=0):
    v = rng.standard_normal(shape, dtype=np.float32) * np.exp2(rng.integers(-12, 13, shape)).astype(np.float32)
    if cols: v *= np.repeat(np.exp2(rng.integers(-cols, cols + 1, shape[:-2] + (1, shape[-1] // 4))) * (rng.random(shape[:-2] + (1, shape[-1] // 4)) > 0.0625), 4, axis=-1).astype(np.float32)
    return mx_ref.flush(v.astype(BF))
T, CAPP, CAPR = 128, 48, 32
def same(t):
    return np.stack([np.concatenate([t, np.zeros((128, 512 - t.shape[1]), BF)], axis=1)] * N)
def bf(t):
    return np.asarray(t, np.float32).astype(BF)
def sized(rng, *shape):
    return 1 + rng.random(shape)
def signs(rng, *shape):
    return 1 - 2 * rng.integers(0, 2, shape)
def setup_inputs(rng):
    return {"x": f(rng, N, 128, 4 * T), "rt": same(f(rng, 128, 4 * N)), "w": f(rng, N, 128, 2048), "u": same(f(rng, 128, 4)), "v": f(rng, N, 128, 512)}
def planted(rng, a, b, own=1.0, off=1.0, way=1):
    d = setup_inputs(rng)
    at = np.arange(128) // (128 // N)
    big, mid = at[None, :, None] == a[:, None, :], at[None, :, None] == b[:, None, :]
    k = np.where(big, 16.0, np.where(mid, 4.0, 1.0))[..., None]
    g = np.where((big | mid)[..., None], 1, signs(rng, N, 128, T, 4))
    d["x"] = bf(sized(rng, N, 128, T, 4) * k * g).reshape(N, 128, 4 * T)
    d["rt"] = same(bf(sized(rng, 128, N, 4) * (at[:, None] == np.arange(N))[..., None]).reshape(128, 4 * N))
    d["w"] = bf(sized(rng, N, 128, 2048) * signs(rng, N, 128, 2048) * np.where(at == np.arange(N)[:, None], own, off)[..., None])
    d["u"] = same(bf(way * sized(rng, 128, 4)))
    return d
def setup_inputs_crowd(rng):
    a, b = np.zeros((N, T), int), np.zeros((N, T), int)
    for s in range(N):
        h, k = (s + (0, 1, 1)[s % 3]) % N, (s + (1, 0, 2)[s % 3]) % N
        rest = rng.permutation(np.array([e for e in range(N) if e not in (h, k)]))
        m, n = rest[np.arange(T) % rest.size], rest[np.arange(1, T + 1) % rest.size]
        p = rng.permutation(T)
        p[:CAPP + 16] = np.sort(p[:CAPP + 16])
        m[:CAPP + 16] = h
        m[CAPP + 16:CAPP + 16 + CAPR] = k
        n[np.concatenate([np.arange(CAPP + 16 + CAPR, T), np.arange(CAPP)])[:CAPP - CAPR]] = k
        a[s, p], b[s, p] = m, n
    return planted(rng, a, b, own=2.0 ** -4, way=-2.0 ** 24)
def setup_inputs_second(rng):
    a, b = np.zeros((N, T), int), np.zeros((N, T), int)
    one, i = int(rng.integers(0, N)), np.arange(T)
    half, last = CAPP // 2, CAPP + CAPP // 2 + 16
    for s in range(N):
        g = rng.permutation(N)
        h, k, rest = g[0], g[1], g[2:]
        m, n = rest[i % rest.size], rest[(i + 1) % rest.size]
        if s == one:
            m[:] = h
            n = g[1 + i % (N - 1)]
        else:
            m[:last] = h
            n[half:last] = k
        turn = (i + rng.integers(0, 2)) % 2 == 1
        p = rng.permutation(T)
        p[:last] = np.sort(p[:last])
        a[s, p], b[s, p] = np.where(turn, m, n), np.where(turn, n, m)
    return planted(rng, a, b, own=2.0 ** 4, way=-1)
def setup_inputs_ties(rng):
    kind = np.stack([rng.permutation(T) % N for s in range(N)])
    e = rng.integers(2, N, (N, T))
    a = np.where(kind == 0, 0, e)
    b = np.where(kind == 0, e, np.where(kind == 1, 0, e ^ 1))
    d = planted(rng, a, b)
    d["rt"][:, :, 4:8] = d["rt"][:, :, :4]
    d["w"][1::2] = d["w"][::2]
    d["w"][:2, :, :4] = 0
    d["w"][1, 128 // N, 0] = BF(4)
    return d
def setup_inputs_zero(rng):
    a = rng.integers(0, N, (N, T))
    b = (a + rng.integers(1, N, (N, T))) % N
    d = planted(rng, a, b, way=-1)
    at, late = np.arange(128) // (128 // N), np.arange(128) % (128 // N) >= 128 // N // 2
    kind = np.stack([rng.permutation(T) % 4 for s in range(N)])
    low = (at[None, :, None] == a[:, None, :]) & (kind % 2 == 1)[:, None, :] | (at[None, :, None] == b[:, None, :]) & (kind >= 2)[:, None, :]
    t = d["x"].astype(np.float32).reshape(N, 128, T, 4)
    d["x"] = bf(np.where(late[None, :, None, None], np.abs(t) * np.where(low, -1, 1)[..., None], t)).reshape(N, 128, 4 * T)
    d["rt"] = bf(d["rt"].astype(np.float32) * ~late[None, :, None])
    d["w"] = bf(np.abs(d["w"].astype(np.float32)) * ((at == np.arange(N)[:, None]) & late)[..., None])
    return d
def setup_inputs_spread(rng):
    return {**setup_inputs(rng), "x": wide(rng, N, 128, 4 * T, cols=6)}
def check_inputs(d):
    b = []
    for k in ("x", "rt", "w", "u", "v"):
        t = np.abs(d[k].astype(np.float32))
        if not (np.isfinite(t).all() and ((t == 0) | (t >= 2.0 ** -30) & (t <= 2.0 ** 30)).all()): b.append("a value of " + k)
    for k, n in (("rt", N), ("u", 1)):
        t = d[k].astype(np.float32)
        if (t[:, :, 4 * n:] != 0).any(): b.append(k + " has numbers behind its first columns")
        if (t != t[:1]).any(): b.append(k + " isn't the same on all ranks")
    return b
def reference(x, rt, w, u, v):
    q, a, b = [], [], []
    for s in range(N):
        q.append(mx_ref.quantize(np.ascontiguousarray(x[s])))
        z = mx_ref.matmul(mx_ref.quantize(np.ascontiguousarray(rt[s])), q[s])[:N] + np.float32(0)
        o = np.argsort(-z, axis=0, kind="stable")
        a.append(o[0])
        b.append(o[1])
    took = [[np.flatnonzero((a[s] == e) | (b[s] == e))[:CAPP] for e in range(N)] for s in range(N)]
    good = np.full((N, N, T), -np.inf, np.float32)
    made = []
    for e in range(N):
        t = join(*[pick(q[s], np.concatenate([took[s][e], np.full(CAPP - took[s][e].size, -1)])) for s in range(N)])
        rs = [mx_ref.matmul(mx_ref.quantize(np.ascontiguousarray(cut(w[e], i))), t) for i in range(4)]
        made.append(mx_ref.quantize(tile([np.maximum(k, np.float32(0)) * np.float32(0.0625) for k in rs])))
        z = mx_ref.matmul(mx_ref.quantize(np.ascontiguousarray(u[e])), made[e])[0] + np.float32(0)
        for s in range(N): good[s, e, took[s][e]] = z[s * CAPP:s * CAPP + took[s][e].size]
    every = join(*made)
    oc, osc = np.zeros((N, 128, 4 * T), np.uint8), np.zeros((N, 16, T), np.uint8)
    wn, y = np.zeros((N, 1, T), np.float32), np.zeros((N, 128, T), np.float32)
    for s in range(N):
        ga, gb = good[s, a[s], np.arange(T)], good[s, b[s], np.arange(T)]
        win = np.where(ga >= gb, a[s], b[s])
        none = np.maximum(ga, gb) == -np.inf
        wn[s, 0] = np.where(none, -100, -1 - win)
        at = np.full(T, -1)
        for e in range(N):
            home = np.flatnonzero((win == e) & ~none)[:CAPR]
            wn[s, 0, home] = e
            at[home] = (e * N + s) * CAPP + np.searchsorted(took[s][e], home)
        z = pick(every, at)
        oc[s], osc[s] = emit(z)
        y[s] = mx_ref.matmul(mx_ref.quantize(np.ascontiguousarray(v[s])), z)
    return {"oc": oc, "osc": osc, "wn": wn, "y": y}

@@ -1,0 +1,445 @@
+from concourse.bass import DstId, RemoteDMATransfer
+from concourse.mybir import dt, AluOpType, AxisListType, ActivationFunctionType
+
+OP, ACT = AluOpType, ActivationFunctionType
+CAPP, CAPR = 48, 32
+HALF = 4 * CAPP
+Z0 = 32
+FW = 144
+TW = 160
+BIG = 9e29
+NV = 7
+
+X4 = "float8_e4m3fn_x4"
+SCRATCH = {
+    "xt": ("sbuf", [128, 520], "bfloat16"), "rtt": ("sbuf", [128, 512], "bfloat16"),
+    "wt": ("sbuf", [128, 2048], "bfloat16"), "ut": ("sbuf", [128, 512], "bfloat16"),
+    "ur": ("sbuf", [128, 512], "bfloat16"), "vt": ("sbuf", [128, 512], "bfloat16"),
+    "ones": ("sbuf", [128, 128], "bfloat16"),
+    "xq": ("sbuf", [128, 130], X4), "xs": ("sbuf", [128, 130], "uint8"),
+    "rq": ("sbuf", [128, 128], X4), "rs": ("sbuf", [128, 128], "uint8"),
+    "wq": ("sbuf", [128, 512], X4), "ws": ("sbuf", [128, 512], "uint8"),
+    "uq": ("sbuf", [128, 128], X4), "us": ("sbuf", [128, 128], "uint8"),
+    "vq": ("sbuf", [128, 128], X4), "vs": ("sbuf", [128, 128], "uint8"),
+    "xd": ("sbuf", [128, 384], X4), "xds": ("sbuf", [128, 384], "uint8"),
+    "xr": ("sbuf", [128, 384], X4), "xrs": ("sbuf", [128, 384], "uint8"),
+    "ht": ("sbuf", [128, 1536], "bfloat16"),
+    "hq": ("sbuf", [128, 384], X4), "hs": ("sbuf", [128, 384], "uint8"),
+    "hr": ("sbuf", [128, 416], X4), "hrs": ("sbuf", [128, 416], "uint8"),
+    "zq": ("sbuf", [128, 128], X4), "zs": ("sbuf", [128, 128], "uint8"),
+    "ps": ("psum", [128, 4096], "float32"),
+    "ci": ("sbuf", [128, 160], "float32"), "cc": ("sbuf", [128, 160], "float32"),
+    "bx": ("sbuf", [128, 160], "float32"), "pm": ("sbuf", [128, 160], "float32"),
+    "zero": ("sbuf", [128, 160], "float32"),
+    "cmp": ("sbuf", [128, 64], "float32"), "junk": ("sbuf", [128, 32], "float32"),
+    "r8": ("sbuf", [128, 8], "float32"), "n4": ("sbuf", [128, 32], "float32"),
+    "f0": ("sbuf", [32, 128], "float32"), "cb": ("sbuf", [32, 128], "bfloat16"),
+    "tmp": ("sbuf", [32, 128 * NV], "bfloat16"), "tms": ("sbuf", [32, 128 * (16 - NV)], "bfloat16"),
+    "lsc": ("sbuf", [32, 16], "float32"), "lt": ("sbuf", [32, 32], "float32"),
+    "of": ("sbuf", [128, 32], "float32"), "off": ("sbuf", [128, 24], "uint16"),
+    "tr": ("sbuf", [128, 32], "float32"), "fr": ("sbuf", [32, 192], "float32"),
+    "rk": ("sbuf", [128, 160], "float32"), "nm": ("sbuf", [128, 160], "float32"),
+    "ct": ("sbuf", [128, 160], "float32"), "tk": ("sbuf", [128, 160], "float32"),
+    "tk2": ("sbuf", [128, 160], "float32"), "rk1": ("sbuf", [128, 160], "float32"),
+    "t2": ("sbuf", [128, 160], "float32"), "role": ("sbuf", [128, 160], "float32"),
+    "p1": ("sbuf", [128, 160], "float32"), "p2": ("sbuf", [128, 160], "float32"),
+    "ma": ("sbuf", [128, 160], "float32"), "mb": ("sbuf", [128, 160], "float32"),
+    "va": ("sbuf", [128, 160], "float32"), "vb": ("sbuf", [128, 160], "float32"),
+    "ta": ("sbuf", [128, 160], "float32"), "tb": ("sbuf", [128, 160], "float32"),
+    "la": ("sbuf", [128, 8], "float32"), "lb": ("sbuf", [128, 8], "float32"),
+    "lo": ("sbuf", [128, 24], "float32"), "le": ("sbuf", [128, 24], "float32"),
+    "lx": ("sbuf", [128, 24], "float32"), "loff": ("sbuf", [128, 24], "uint16"),
+    "qw": ("sbuf", [128, 416], "float32"),
+    "ga": ("sbuf", [128, 144], "float32"), "gb": ("sbuf", [128, 144], "float32"),
+    "dd": ("sbuf", [128, 144], "float32"), "win": ("sbuf", [128, 144], "float32"),
+    "cw": ("sbuf", [128, 144], "float32"), "hf": ("sbuf", [128, 144], "float32"),
+    "xp": ("sbuf", [128, 144], "float32"), "val": ("sbuf", [128, 160], "float32"),
+    "tv": ("sbuf", [128, 160], "float32"), "s8": ("sbuf", [128, 8], "float32"),
+    "zoff": ("sbuf", [128, 8], "uint16"),
+    "wa": ("sbuf", [32, 8], "float32"), "we": ("sbuf", [32, 8], "int32"), "ww": ("sbuf", [32, 8], "float32"),
+    "wf": ("sbuf", [32, 8], "float32"), "wh": ("sbuf", [32, 8], "float32"), "wg": ("sbuf", [32, 8], "float32"),
+    "wz": ("sbuf", [32, 8], "float32"), "wk": ("sbuf", [32, 8], "float32"), "wm": ("sbuf", [32, 8], "float32"),
+    "wj": ("sbuf", [32, 8], "float32"), "wn4": ("sbuf", [32, 32], "float32"), "wnt": ("sbuf", [32, 32], "float32"),
+    "ysb": ("sbuf", [128, 128], "float32"),
+}
+DMAS = ["dx", "drt", "dw0", "dw1", "du", "dv", "dxo", "dxos", "dz", "dzs", "dho", "dhos", "doc", "dos0", "dos1", "dos2",
+        "dos3", "dy", "dwn"]
+SEMAPHORES = ["cv", "cs", "ct", "cg", "ls", "xa1", "xa2", "ha1", "ha2"] + DMAS
+BANK = 512
+
+
+def _runner(g, T):
+    queues = {"v": g.vector, "s": g.scalar, "t": g.tensor, "g": g, "y": g.sync}
+    own = {"v": "cv", "s": "cs", "t": "ct", "g": "cg"}
+    total, known, snap, recs = {}, {q: {} for q in queues}, {}, {}
+
+    def region(view):
+        b, p0, p1, c0, c1, st = view
+        if SCRATCH[b][0] == "psum":
+            return (0, 128, c0 // BANK * BANK, -(-c1 // BANK) * BANK, 1)
+        return (p0, p1, c0, c1, st)
+
+    def meet(a, b):
+        if a[0] >= b[1] or b[0] >= a[1] or a[2] >= b[3] or b[2] >= a[3]:
+            return False
+        return not (a[4] > 1 and a[4] == b[4] and (a[2] - b[2]) % a[4])
+
+    def wait_for(q, need):
+        need = [(s, v) for s, v in need.items() if known[q].get(s, 0) < v]
+        for i, (s, v) in enumerate(need):
+            if any(snap.get(o, {}).get(s, 0) >= v for j, o in enumerate(need) if j != i):
+                continue
+            queues[q].wait_ge(T.sem[s], v)
+        for s, v in need:
+            known[q][s] = max(known[q].get(s, 0), v)
+            for s2, v2 in snap.get((s, v), {}).items():
+                known[q][s2] = max(known[q].get(s2, 0), v2)
+
+    def wants(q, outs, ins):
+        need = {}
+        for wr, views in ((True, outs), (False, ins)):
+            for view in views:
+                r = region(view)
+                ps = SCRATCH[view[0]][0] == "psum"
+                for w, r2, tok, q2 in recs.get(view[0], []):
+                    if not (wr or w or (ps and q2 != q)) or not meet(r, r2):
+                        continue
+                    need[tok[0]] = max(need.get(tok[0], 0), tok[1])
+        return need
+
+    def note(q, outs, ins, tok):
+        for wr, views in ((True, outs), (False, ins)):
+            for view in views:
+                recs.setdefault(view[0], []).append((wr, region(view), tok, q))
+
+    def op(q, call, outs, ins, dma=None):
+        wait_for(q, wants(q, outs, ins))
+        sem, n = (dma, 16) if dma else (own[q], 1)
+        call(queues[q]).then_inc(T.sem[sem], n)
+        total[sem] = total.get(sem, 0) + n
+        tok = (sem, total[sem])
+        snap[tok] = dict(known[q])
+        note(q, outs, ins, tok)
+
+    def arrive(sem, n, outs):
+        total[sem] = total.get(sem, 0) + n
+        note("far", outs, [], (sem, total[sem]))
+
+    def send(call, ins, ls):
+        wait_for("g", wants("g", [], ins))
+        call(g)
+        total["ls"] = total.get("ls", 0) + ls
+
+    def finish():
+        wait_for("g", dict(total))
+
+    return op, arrive, send, finish
+
+
+def rank_program(g, core, T, topo):
+    rank = T.rank_of(core)
+    if rank is None:
+        return
+    op, arrive, send, finish = _runner(g, T)
+    N = len(T.cores)
+
+    chips = []
+    for c in T.cores:
+        if topo.chip(c) not in chips:
+            chips.append(topo.chip(c))
+    on = [[r for r in range(N) if topo.chip(T.cores[r]) == ch] for ch in chips]
+
+    def place(r):
+        return next(i for i in range(len(on)) if r in on[i])
+
+    def experts(r):
+        return [e for i in range(len(on)) for e in on[(place(r) + i) % len(on)]]
+
+    def sources(r):
+        return [e for i in range(len(on)) for e in on[(place(r) - i) % len(on)]]
+
+    EXP, SRC = experts(rank), sources(rank)
+    base = EXP[0]
+    mine = EXP.index(rank)
+    mine_src = SRC.index(rank)
+    away = topo.engines(core, next(c for c in T.cores if topo.chip(c) != topo.chip(core)))
+    peer = next(c for c in T.cores if topo.chip(c) == topo.chip(core) and c != core)
+    near = [e for e in topo.engines(core, peer) if e not in away][:2]
+
+    def V(b, c0=0, c1=None, p0=0, p1=None, st=1):
+        sh = SCRATCH[b][1]
+        return (b, p0, sh[0] if p1 is None else p1, c0, sh[1] if c1 is None else c1, st)
+
+    def ap(v):
+        b, p0, p1, c0, c1, st = v
+        return T[b][p0:p1, c0:c1] if st == 1 else T[b][p0:p1, c0:c1:st]
+
+    def by(v):
+        return ap(v).bitcast(dt.uint8)
+
+    def memset(v, x):
+        op("v", lambda q: q.memset(ap(v), x), [v], [])
+
+    def copy(out, in_, q="v"):
+        if q == "v":
+            op("v", lambda e: e.tensor_copy(ap(out), ap(in_)), [out], [in_])
+        else:
+            op("s", lambda e: e.activation(ap(out), ap(in_), ACT.Copy), [out], [in_])
+
+    def tt(out, a, b, o):
+        op("v", lambda q: q.tensor_tensor(ap(out), ap(a), ap(b), o), [out], [a, b])
+
+    def ts(out, a, s1, o1, s2=None, o2=None):
+        ins = [a] + [s for s in (s1, s2) if isinstance(s, tuple)]
+        x1, x2 = (ap(s) if isinstance(s, tuple) else s for s in (s1, s2))
+        if o2 is None:
+            op("v", lambda q: q.tensor_scalar(ap(out), ap(a), x1, None, o1), [out], ins)
+        else:
+            op("v", lambda q: q.tensor_scalar(ap(out), ap(a), x1, x2, o1, o2), [out], ins)
+
+    def total(out, in_, q="v", junk=None):
+        if q == "v":
+            op("v", lambda e: e.tensor_reduce(ap(out), ap(in_), AxisListType.X, OP.add), [out], [in_])
+        else:
+            op("s", lambda e: e.activation(ap(junk), ap(in_), ACT.Identity, accum_out=ap(out)), [out, junk], [in_])
+
+    def scan(out, a, b, init):
+        ini = ap(init) if isinstance(init, tuple) else init
+        op("v", lambda q: q.tensor_tensor_scan(ap(out), ap(a), ap(b), ini, OP.add, OP.add), [out],
+           [a, b] + ([init] if isinstance(init, tuple) else []))
+
+    def turn(out, in_):
+        op("v", lambda q: q.transpose(ap(out), ap(in_)), [out], [in_])
+
+    def quant(c, s, t):
+        op("v", lambda q: q.quantize_mx(ap(c), ap(s), ap(t)), [c, s], [t])
+
+    def mm(col, n, lc, ls, rc, rs):
+        out = V("ps", col, col + n)
+        op("t", lambda q: q.matmul_mx(ap(out), ap(lc), ap(ls), ap(rc), ap(rs), True, True), [out], [lc, ls, rc, rs])
+
+    def pick(oc, os, wc, ws, lst):
+        op("v", lambda q: q.tensor_copy(ap(oc).bitcast(dt.uint32), ap(wc).bitcast(dt.uint32).indirect(ap(lst))), [oc], [wc, lst])
+        op("s", lambda q: q.activation(ap(os), ap(ws).indirect(ap(lst)), ACT.Copy), [os], [ws, lst])
+
+    def load(q, sem, out, src):
+        op(q, lambda e: e.dma_start(ap(out), src), [out], [], dma=sem)
+
+    def move(q, sem, out, in_, codes):
+        f = by if codes else ap
+        op(q, lambda e: e.dma_start(f(out), f(in_)), [out], [in_], dma=sem)
+
+    def store(q, sem, dst, in_, codes=False):
+        f = by if codes else ap
+        op(q, lambda e: e.dma_start(dst, f(in_)), [], [in_], dma=sem)
+
+    load("y", "dx", V("xt", 0, 512), T.x[:, :])
+    load("s", "drt", V("rtt"), T.rt[:, :])
+    load("y", "dw0", V("wt", 0, 1024), T.w[:, 0:1024])
+    load("s", "dw1", V("wt", 1024, 2048), T.w[:, 1024:2048])
+    load("y", "du", V("ut"), T.u[:, :])
+    load("y", "dv", V("vt"), T.v[:, :])
+
+    def iota(v, pattern, b):
+        op("g", lambda q: q.iota(ap(v), pattern, b, 0, allow_small_or_imprecise_dtypes=True), [v], [])
+
+    iota(V("ci", 0, 24), [[0, 8], [-16, 3]], 0)
+    iota(V("ci", 24, 32), [[0, 8]], 0)
+    iota(V("ci", 32, 64), [[0, 4], [CAPP, 8]], Z0 - 1)
+    iota(V("ci", 64, 96), [[-1, 2], [0, 16]], 1)
+    iota(V("ci", 96, 128), [[1, 2], [0, 16]], 0)
+    iota(V("ci", 128, 160), [[0, 2], [1, 2], [0, 8]], 0)
+    iota(V("bx"), [[0, 5], [1, 2], [0, 16]], 0)
+    memset(V("xt", 512, 520), 0.0)
+    memset(V("zero"), 0.0)
+    memset(V("n4", 24, 32), 0.0)
+    memset(V("fr"), 8.0)
+    memset(V("qw", 0, Z0), -BIG)
+    memset(V("val", FW, TW), 0.0)
+    memset(V("lo"), 0.0)
+    memset(V("le"), 0.0)
+    memset(V("wn4"), 0.0)
+    memset(V("ones"), 1.0)
+    turn(V("cc"), V("ci"))
+    kcol = V("cc", 0, 1, 0, 32)
+    ecol, even, odd, hcol = V("cc", 32, 33), V("cc", 64, 65), V("cc", 96, 97), V("cc", 128, 129)
+    ts(V("pm"), V("bx"), hcol, OP.is_equal)
+
+    quant(V("rq"), V("rs"), V("rtt"))
+    quant(V("xq"), V("xs"), V("xt"))
+    mm(0, 128, V("xq", 0, 128), V("xs", 0, 128), V("rq"), V("rs"))
+    for e in (4, 5, 6, 7, 0, 1, 2, 3):
+        sc = V("ps", e, e + 1)
+        if e:
+            ts(V("cmp", 8 * e, 8 * e + e), V("ps", 0, e), sc, OP.is_ge)
+        ts(V("cmp", 9 * e, 8 * e + 8), V("ps", e, 8), sc, OP.is_gt)
+    for e in range(8):
+        i = EXP.index(e)
+        total(V("r8", i, i + 1), V("cmp", 8 * e, 8 * e + 8), "v" if e < 4 else "s", V("junk", 8 * (e % 4), 8 * (e % 4) + 8))
+    for k in range(3):
+        ts(V("n4", k, 24, st=3), V("r8"), 1.0, OP.is_le)
+    for a in range(4):
+        turn(V("f0", 32 * a, 32 * a + 32), V("n4", 0, 32, 32 * a, 32 * a + 32))
+    scan(V("cb"), V("f0"), V("zero", 0, 128, 0, 32), kcol)
+    for m in range(NV, 16):
+        j = V("tms", 128 * (m - NV), 128 * (m - NV) + 128)
+        acc = V("lsc", m, m + 1)
+        bias = m + 0.5
+        op("s", lambda q: q.activation(ap(j), ap(V("cb")), ACT.Sign, bias=bias, scale=-1.0, accum_out=ap(acc)), [j, acc], [V("cb")])
+    for m in range(NV):
+        ts(V("tmp", 128 * m, 128 * m + 128), V("cb"), float(m), OP.is_le)
+    for m in range(NV):
+        total(V("lt", m, m + 1), V("tmp", 128 * m, 128 * m + 128))
+    copy(V("lt", 16, 16 + NV), V("lt", 0, NV))
+    ts(V("lt", NV, 16), V("lsc", NV, 16), 0.5, OP.mult, 64.0, OP.add)
+    ts(V("lt", 16 + NV, 32), V("lsc", NV, 16), 0.5, OP.mult, 64.0, OP.add)
+    for a in range(4):
+        turn(V("of", 0, 32, 32 * a, 32 * a + 32), V("lt"))
+    copy(V("off"), V("of", 0, 24))
+
+    def engines_of(n):
+        k = len(away) // n
+        return [sum(1 << x for x in away[k * i:k * i + k]) for i in range(n)], k
+
+    def ship(order, half, src, dst, sem, col_of, width, codes, off0=0, soff0=0):
+        f = by if codes else ap
+        to = [(i, T.cores[order[i]]) for i in range(4 * half, 4 * half + 4) if order[i] != rank]
+        far = [x for x in to if topo.chip(x[1]) != topo.chip(core)]
+        masks, k = engines_of(len(far))
+        trs, ins, ls = [], [], 0
+        for i, c in to:
+            if (i, c) in far:
+                mask, n = masks[far.index((i, c))], k
+            else:
+                mask, n = sum(1 << x for x in near), len(near)
+            rid, pid, _s = topo.addr(c)
+            s = V(src, soff0 + CAPP * i, soff0 + CAPP * i + CAPP)
+            at = off0 + CAPP * col_of(T.rank_of(c))
+            d = V(dst, at, at + CAPP)
+            trs.append(RemoteDMATransfer(dst_ids=[DstId(rid=rid, pnc=pid)], dma_engine_mask=mask, remote_sem=T.sem[sem],
+                                         src=f(s), dst=f(d)))
+            ins.append(s)
+            ls += n
+        send(lambda q: q.remote_dma_fused(trs, local_sem=T.sem["ls"]), ins, ls)
+
+    def landed(half):
+        far = 2 if half == 0 else 4
+        return 2 * (far * (len(away) // far) + (len(near) if half == 0 else 0))
+
+    for h in range(2):
+        a, b = HALF * h, HALF * h + HALF
+        pick(V("xd", a, b), V("xds", a, b), V("xq"), V("xs"), V("off", 12 * h, 12 * h + 12))
+        ship(EXP, h, "xd", "xr", "xa%d" % (h + 1), lambda r: sources(r).index(rank), CAPP, True)
+        ship(EXP, h, "xds", "xrs", "xa%d" % (h + 1), lambda r: sources(r).index(rank), CAPP, False)
+        if h == 0:
+            m, n = CAPP * mine, CAPP * mine_src
+            move("y", "dxo", V("xr", n, n + CAPP), V("xd", m, m + CAPP), True)
+            move("y", "dxos", V("xrs", n, n + CAPP), V("xds", m, m + CAPP), False)
+            move("y", "dz", V("hr", 0, 2), V("xq", 128, 130), True)
+            move("y", "dzs", V("hrs", 0, 2), V("xs", 128, 130), False)
+    for h in range(2):
+        for i in range(4 * h, 4 * h + 4):
+            if SRC[i] != rank:
+                arrive("xa%d" % (h + 1), 0, [V("xr", CAPP * i, CAPP * i + CAPP), V("xrs", CAPP * i, CAPP * i + CAPP)])
+
+    quant(V("wq"), V("ws"), V("wt"))
+    for j in range(4):
+        copy(V("tr", 8 * j, 8 * j + 8), V("r8"), "s")
+    for a in range(4):
+        turn(V("fr", 32 + 32 * a, 64 + 32 * a), V("tr", 0, 32, 32 * a, 32 * a + 32))
+    for a in range(4):
+        copy(V("rk", 0, TW, 32 * a, 32 * a + 32), V("fr", 32, 192), "s")
+        copy(V("rk", 0, TW, 32 * a, 32 * a + 16), V("fr", 16, 176, 0, 16), "s")
+    ts(V("nm"), V("rk"), 1.0, OP.is_le)
+    ts(V("rk1"), V("rk"), 1.0, OP.add)
+    scan(V("ct"), V("nm"), V("zero"), 0.0)
+    ts(V("tk"), V("ct"), float(CAPP), OP.is_le)
+    ts(V("p1"), V("ct"), ecol, OP.add, 2.0, OP.mult)
+    tt(V("tk2"), V("tk"), V("nm"), OP.mult)
+    tt(V("p2"), V("p1"), V("pm"), OP.mult)
+    tt(V("t2"), V("tk2"), V("rk1"), OP.mult)
+    ts(V("role"), V("t2"), 1.0, OP.subtract)
+
+    for h in range(2):
+        a, b = HALF * h, HALF * h + HALF
+        arrive("xa%d" % (h + 1), landed(h), [V("xr", c, c + CAPP) for c in range(a, b, CAPP) if c != CAPP * mine_src]
+               + [V("xrs", c, c + CAPP) for c in range(a, b, CAPP) if c != CAPP * mine_src])
+        for i in (0, 2, 1, 3):
+            w = V("wq", 128 * i, 128 * i + 128), V("ws", 128 * i, 128 * i + 128)
+            mm(BANK * (4 * h + i), HALF, w[0], w[1], V("xr", a, b), V("xrs", a, b))
+        for i in range(4):
+            r, o = V("ps", BANK * (4 * h + i), BANK * (4 * h + i) + HALF), V("ht", 4 * a + i, 4 * b, st=4)
+            if i < 2:
+                ts(o, r, 0.0, OP.max, 0.0625, OP.mult)
+            else:
+                op("s", lambda q: q.activation(ap(o), ap(r), ACT.Relu, scale=0.0625), [o], [r])
+        quant(V("hq", a, b), V("hs", a, b), V("ht", 4 * a, 4 * b))
+        ship(SRC, h, "hq", "hr", "ha%d" % (h + 1), lambda r: experts(r).index(rank), CAPP, True, Z0)
+        ship(SRC, h, "hs", "hrs", "ha%d" % (h + 1), lambda r: experts(r).index(rank), CAPP, False, Z0)
+        if h == 0:
+            n, m = CAPP * mine_src, Z0 + CAPP * mine
+            move("y", "dho", V("hr", m, m + CAPP), V("hq", n, n + CAPP), True)
+            move("y", "dhos", V("hrs", m, m + CAPP), V("hs", n, n + CAPP), False)
+
+    for t in range(4):
+        ts(V("ur", t, 512, st=4), V("ones"), V("ut", t, t + 1), OP.mult)
+    quant(V("uq"), V("us"), V("ur"))
+    quant(V("vq"), V("vs"), V("vt"))
+    ts(V("ma"), V("t2"), 1.0, OP.is_equal, 0.5, OP.mult)
+    ts(V("mb"), V("t2"), 2.0, OP.is_equal, 0.5, OP.mult)
+    tt(V("va"), V("ma"), V("p2"), OP.mult)
+    tt(V("vb"), V("mb"), V("p2"), OP.mult)
+    turn(V("ta"), V("va"))
+    turn(V("tb"), V("vb"))
+    for k in range(8):
+        total(V("la", k, k + 1), V("ta", 16 * k + 8, 16 * k + 24))
+        total(V("lb", k, k + 1), V("tb", 16 * k + 8, 16 * k + 24), "s", V("junk", 16 * (k % 2), 16 * (k % 2) + 16))
+    for j, l in ((0, "la"), (12, "lb")):
+        ts(V("lo", j, j + 8), V(l), odd, OP.mult)
+        ts(V("le", j + 1, j + 9), V(l), even, OP.mult)
+    tt(V("lx"), V("lo"), V("le"), OP.add)
+    copy(V("loff"), V("lx"))
+
+    for h in range(2):
+        a, b = Z0 + HALF * h, Z0 + HALF * h + HALF
+        skip = Z0 + CAPP * mine
+        arrive("ha%d" % (h + 1), landed(h), [V("hr", c, c + CAPP) for c in range(a, b, CAPP) if c != skip]
+               + [V("hrs", c, c + CAPP) for c in range(a, b, CAPP) if c != skip])
+        mm(BANK * h, HALF, V("uq"), V("us"), V("hr", a, b), V("hrs", a, b))
+        copy(V("qw", a, b), V("ps", BANK * h, BANK * h + HALF), "s" if h == 0 else "v")
+    lsta, lstb = V("loff", 0, 9), V("loff", 12, 21)
+    op("v", lambda q: q.tensor_copy(ap(V("ga")), ap(V("qw")).indirect(ap(lsta))), [V("ga")], [V("qw"), lsta])
+    op("s", lambda q: q.activation(ap(V("gb")), ap(V("qw")).indirect(ap(lstb)), ACT.Copy), [V("gb")], [V("qw"), lstb])
+    tt(V("dd"), V("gb"), V("ga"), OP.is_gt)
+    tt(V("win"), V("dd"), V("role", 0, FW), OP.is_equal)
+    scan(V("cw"), V("win"), V("zero", 0, FW), 0.0)
+    tt(V("xp"), V("win"), V("p2", 0, FW), OP.mult)
+    ts(V("hf"), V("cw"), float(CAPR), OP.is_le, 0.5, OP.subtract)
+    tt(V("val", 0, FW), V("xp"), V("hf"), OP.mult)
+    turn(V("tv"), V("val"))
+    for k in range(8):
+        total(V("s8", k, k + 1), V("tv", 16 * k + 8, 16 * k + 24), "v" if k < 5 else "s", V("junk", 16 * (k % 2), 16 * (k % 2) + 16))
+    copy(V("zoff"), V("s8"))
+    pick(V("zq"), V("zs"), V("hr"), V("hrs"), V("zoff"))
+    mm(BANK * 2, 128, V("vq"), V("vs"), V("zq"), V("zs"))
+    store("y", "doc", T.oc[:, :], V("zq"), True)
+    for k in range(4):
+        store("y", "dos%d" % k, T.osc[4 * k:4 * k + 4, :], V("zs", 0, 128, 32 * k, 32 * k + 4))
+    s = V("s8", 0, 8, 0, 32)
+    op("s", lambda q: q.activation(ap(V("wa")), ap(s), ACT.Abs), [V("wa")], [s])
+    ts(V("wh"), s, 1.0, OP.is_ge)
+    ts(V("wz"), s, 0.0, OP.is_equal, float(base - 100), OP.mult)
+    ts(V("wg"), V("wh"), 2.0, OP.mult, 1.0, OP.subtract)
+    ts(V("wk"), V("wh"), 1.0, OP.subtract)
+    mid = Z0 + (CAPP - 1) / 2.0
+    ts(V("we"), V("wa"), 1.0 / CAPP, OP.mult, base - mid / CAPP, OP.add)
+    tt(V("wj"), V("wz"), V("wk"), OP.add)
+    ts(V("ww"), V("we"), float(N), OP.is_ge, -float(N), OP.mult)
+    tt(V("wf"), V("we"), V("ww"), OP.add)
+    tt(V("wm"), V("wf"), V("wg"), OP.mult)
+    tt(V("wn4", 0, 8), V("wm"), V("wj"), OP.add)
+    turn(V("wnt"), V("wn4"))
+    copy(V("ysb"), V("ps", BANK * 2, BANK * 2 + 128), "s")
+    store("s", "dy", T.y[:, :], V("ysb"))
+    store("y", "dwn", T.wn[:, :], V("wnt", 0, 16, 0, 8))
+    finish()

@@ -8,64 +8,31 @@ Z0 = 32
 FW = 144
 TW = 160
 BIG = 9e29
-NV = 7
+BANK = 512
 
-X4 = "float8_e4m3fn_x4"
-SCRATCH = {
-    "xt": ("sbuf", [128, 520], "bfloat16"), "rtt": ("sbuf", [128, 512], "bfloat16"),
-    "wt": ("sbuf", [128, 2048], "bfloat16"), "ut": ("sbuf", [128, 512], "bfloat16"),
-    "ur": ("sbuf", [128, 512], "bfloat16"), "vt": ("sbuf", [128, 512], "bfloat16"),
-    "ones": ("sbuf", [128, 128], "bfloat16"),
-    "xq": ("sbuf", [128, 130], X4), "xs": ("sbuf", [128, 130], "uint8"),
-    "rq": ("sbuf", [128, 128], X4), "rs": ("sbuf", [128, 128], "uint8"),
-    "wq": ("sbuf", [128, 512], X4), "ws": ("sbuf", [128, 512], "uint8"),
-    "uq": ("sbuf", [128, 128], X4), "us": ("sbuf", [128, 128], "uint8"),
-    "vq": ("sbuf", [128, 128], X4), "vs": ("sbuf", [128, 128], "uint8"),
-    "xd": ("sbuf", [128, 384], X4), "xds": ("sbuf", [128, 384], "uint8"),
-    "xr": ("sbuf", [128, 384], X4), "xrs": ("sbuf", [128, 384], "uint8"),
-    "ht": ("sbuf", [128, 1536], "bfloat16"),
-    "hq": ("sbuf", [128, 384], X4), "hs": ("sbuf", [128, 384], "uint8"),
-    "hr": ("sbuf", [128, 416], X4), "hrs": ("sbuf", [128, 416], "uint8"),
-    "zq": ("sbuf", [128, 128], X4), "zs": ("sbuf", [128, 128], "uint8"),
-    "ps": ("psum", [128, 4096], "float32"),
-    "ci": ("sbuf", [128, 160], "float32"), "cc": ("sbuf", [128, 160], "float32"),
-    "bx": ("sbuf", [128, 160], "float32"), "pm": ("sbuf", [128, 160], "float32"),
-    "zero": ("sbuf", [128, 160], "float32"),
-    "cmp": ("sbuf", [128, 64], "float32"), "junk": ("sbuf", [128, 32], "float32"),
-    "r8": ("sbuf", [128, 8], "float32"), "n4": ("sbuf", [128, 32], "float32"),
-    "f0": ("sbuf", [32, 128], "float32"), "cb": ("sbuf", [32, 128], "bfloat16"),
-    "tmp": ("sbuf", [32, 128 * NV], "bfloat16"), "tms": ("sbuf", [32, 128 * (16 - NV)], "bfloat16"),
-    "lsc": ("sbuf", [32, 16], "float32"), "lt": ("sbuf", [32, 32], "float32"),
-    "of": ("sbuf", [128, 32], "float32"), "off": ("sbuf", [128, 24], "uint16"),
-    "tr": ("sbuf", [128, 32], "float32"), "fr": ("sbuf", [32, 192], "float32"),
-    "rk": ("sbuf", [128, 160], "float32"), "nm": ("sbuf", [128, 160], "float32"),
-    "ct": ("sbuf", [128, 160], "float32"), "tk": ("sbuf", [128, 160], "float32"),
-    "tk2": ("sbuf", [128, 160], "float32"), "rk1": ("sbuf", [128, 160], "float32"),
-    "t2": ("sbuf", [128, 160], "float32"), "role": ("sbuf", [128, 160], "float32"),
-    "p1": ("sbuf", [128, 160], "float32"), "p2": ("sbuf", [128, 160], "float32"),
-    "ma": ("sbuf", [128, 160], "float32"), "mb": ("sbuf", [128, 160], "float32"),
-    "va": ("sbuf", [128, 160], "float32"), "vb": ("sbuf", [128, 160], "float32"),
-    "ta": ("sbuf", [128, 160], "float32"), "tb": ("sbuf", [128, 160], "float32"),
-    "la": ("sbuf", [128, 8], "float32"), "lb": ("sbuf", [128, 8], "float32"),
-    "lo": ("sbuf", [128, 24], "float32"), "le": ("sbuf", [128, 24], "float32"),
-    "lx": ("sbuf", [128, 24], "float32"), "loff": ("sbuf", [128, 24], "uint16"),
-    "qw": ("sbuf", [128, 416], "float32"),
-    "ga": ("sbuf", [128, 144], "float32"), "gb": ("sbuf", [128, 144], "float32"),
-    "dd": ("sbuf", [128, 144], "float32"), "win": ("sbuf", [128, 144], "float32"),
-    "cw": ("sbuf", [128, 144], "float32"), "hf": ("sbuf", [128, 144], "float32"),
-    "xp": ("sbuf", [128, 144], "float32"), "val": ("sbuf", [128, 160], "float32"),
-    "tv": ("sbuf", [128, 160], "float32"), "s8": ("sbuf", [128, 8], "float32"),
-    "zoff": ("sbuf", [128, 8], "uint16"),
-    "wa": ("sbuf", [32, 8], "float32"), "we": ("sbuf", [32, 8], "int32"), "ww": ("sbuf", [32, 8], "float32"),
-    "wf": ("sbuf", [32, 8], "float32"), "wh": ("sbuf", [32, 8], "float32"), "wg": ("sbuf", [32, 8], "float32"),
-    "wz": ("sbuf", [32, 8], "float32"), "wk": ("sbuf", [32, 8], "float32"), "wm": ("sbuf", [32, 8], "float32"),
-    "wj": ("sbuf", [32, 8], "float32"), "wn4": ("sbuf", [32, 32], "float32"), "wnt": ("sbuf", [32, 32], "float32"),
-    "ysb": ("sbuf", [128, 128], "float32"),
-}
+SCRATCH = {"ps": ("psum", [128, 8 * BANK], "float32"), "we": ("sbuf", [32, 8], "int32"), "f0": ("sbuf", [32, 128], "float32"),
+           "lt": ("sbuf", [32, 32], "float32"), "fr": ("sbuf", [32, 192], "float32"), "wn4": ("sbuf", [32, 32], "float32"),
+           "wnt": ("sbuf", [32, 32], "float32"), "wa": ("sbuf", [32, 8], "float32"), "wh": ("sbuf", [32, 8], "float32"),
+           "wz": ("sbuf", [32, 8], "float32"), "off": ("sbuf", [128, 24], "uint16"), "loff": ("sbuf", [128, 24], "uint16"),
+           "zoff": ("sbuf", [128, 8], "uint16")}
+for _n, _w in (("xt", 520), ("rtt", 512), ("wt", 2048), ("ut", 512), ("ur", 512), ("vt", 512), ("ones", 128), ("ht", 1536),
+               ("cb", 128), ("tmp", 256), ("tms", 256)):
+    SCRATCH[_n] = ("sbuf", [128, _w], "bfloat16")
+for _n, _w in (("xq", 130), ("rq", 128), ("wq", 512), ("uq", 128), ("vq", 128), ("xd", 384), ("xr", 384), ("hq", 384),
+               ("hr", 416), ("zq", 128)):
+    SCRATCH[_n] = ("sbuf", [128, _w], "float8_e4m3fn_x4")
+    SCRATCH[_n + "s"] = ("sbuf", [128, _w], "uint8")
+for _n, _w in (("ci", 192), ("cc", 192), ("sc", 1), ("bx", TW), ("pm", TW), ("zero", TW),
+               ("cmp", 64), ("junk", 160), ("r8", 8), ("n4", 32), ("lc", 4), ("of", 32),
+               ("tr", 32), ("rk", TW), ("nm", TW), ("ct", TW), ("tk", TW), ("tk2", TW), ("rk1", TW), ("t2", TW), ("role", TW),
+               ("p1", TW), ("p2", TW), ("ma", TW), ("mb", TW), ("va", TW), ("vb", TW), ("ta", TW), ("tb", TW),
+               ("la", 8), ("lb", 8), ("lo", 24), ("le", 24), ("lx", 24),
+               ("qw", 416), ("yw", 416), ("ga", FW), ("gb", FW), ("dd", FW), ("win", FW), ("cw", FW), ("hf", FW), ("xp", FW),
+               ("val", TW), ("tv", TW), ("s8", 8), ("ysb", 128)):
+    SCRATCH[_n] = ("sbuf", [128, _w], "float32")
 DMAS = ["dx", "drt", "dw0", "dw1", "du", "dv", "dxo", "dxos", "dz", "dzs", "dho", "dhos", "doc", "dos0", "dos1", "dos2",
         "dos3", "dy", "dwn"]
-SEMAPHORES = ["cv", "cs", "ct", "cg", "ls", "xa1", "xa2", "ha1", "ha2"] + DMAS
-BANK = 512
+SEMAPHORES = ["cv", "cs", "ct", "cg", "ls", "xa0", "xa1", "ha0", "ha1"] + DMAS
 
 
 def _runner(g, T):
@@ -143,28 +110,15 @@ def rank_program(g, core, T, topo):
     op, arrive, send, finish = _runner(g, T)
     N = len(T.cores)
 
-    chips = []
-    for c in T.cores:
-        if topo.chip(c) not in chips:
-            chips.append(topo.chip(c))
-    on = [[r for r in range(N) if topo.chip(T.cores[r]) == ch] for ch in chips]
-
-    def place(r):
-        return next(i for i in range(len(on)) if r in on[i])
-
-    def experts(r):
-        return [e for i in range(len(on)) for e in on[(place(r) + i) % len(on)]]
-
-    def sources(r):
-        return [e for i in range(len(on)) for e in on[(place(r) - i) % len(on)]]
-
-    EXP, SRC = experts(rank), sources(rank)
-    base = EXP[0]
-    mine = EXP.index(rank)
-    mine_src = SRC.index(rank)
+    chip = [topo.chip(c) for c in T.cores]
+    first = rank // 4
+    batch = [[4 * (first ^ h) + i for i in range(4)] for h in range(2)]
     away = topo.engines(core, next(c for c in T.cores if topo.chip(c) != topo.chip(core)))
     peer = next(c for c in T.cores if topo.chip(c) == topo.chip(core) and c != core)
     near = [e for e in topo.engines(core, peer) if e not in away][:2]
+
+    def bits(es):
+        return sum(1 << e for e in es)
 
     def V(b, c0=0, c1=None, p0=0, p1=None, st=1):
         sh = SCRATCH[b][1]
@@ -180,11 +134,16 @@ def rank_program(g, core, T, topo):
     def memset(v, x):
         op("v", lambda q: q.memset(ap(v), x), [v], [])
 
+    def act(out, in_, f, lst=None, acc=None, **k):
+        src = ap(in_) if lst is None else ap(in_).indirect(ap(lst))
+        kk = dict(k) if acc is None else dict(k, accum_out=ap(acc))
+        op("s", lambda q: q.activation(ap(out), src, f, **kk), [out] + ([acc] if acc else []), [in_] + ([lst] if lst else []))
+
     def copy(out, in_, q="v"):
         if q == "v":
             op("v", lambda e: e.tensor_copy(ap(out), ap(in_)), [out], [in_])
         else:
-            op("s", lambda e: e.activation(ap(out), ap(in_), ACT.Copy), [out], [in_])
+            act(out, in_, ACT.Copy)
 
     def tt(out, a, b, o):
         op("v", lambda q: q.tensor_tensor(ap(out), ap(a), ap(b), o), [out], [a, b])
@@ -197,11 +156,11 @@ def rank_program(g, core, T, topo):
         else:
             op("v", lambda q: q.tensor_scalar(ap(out), ap(a), x1, x2, o1, o2), [out], ins)
 
-    def total(out, in_, q="v", junk=None):
+    def total(out, in_, q="v", at=0):
         if q == "v":
             op("v", lambda e: e.tensor_reduce(ap(out), ap(in_), AxisListType.X, OP.add), [out], [in_])
         else:
-            op("s", lambda e: e.activation(ap(junk), ap(in_), ACT.Identity, accum_out=ap(out)), [out, junk], [in_])
+            act(V("junk", at, at + in_[4] - in_[3]), in_, ACT.Identity, acc=out)
 
     def scan(out, a, b, init):
         ini = ap(init) if isinstance(init, tuple) else init
@@ -211,34 +170,31 @@ def rank_program(g, core, T, topo):
     def turn(out, in_):
         op("v", lambda q: q.transpose(ap(out), ap(in_)), [out], [in_])
 
-    def quant(c, s, t):
-        op("v", lambda q: q.quantize_mx(ap(c), ap(s), ap(t)), [c, s], [t])
+    def quant(c, t, a=0, b=None):
+        o, s, i = V(c, a, b), V(c + "s", a, b), V(t, 4 * a, None if b is None else 4 * b)
+        op("v", lambda q: q.quantize_mx(ap(o), ap(s), ap(i)), [o, s], [i])
 
-    def mm(col, n, lc, ls, rc, rs):
-        out = V("ps", col, col + n)
+    def mm(bank, l, la, r, ra, rb):
+        out, lc, ls, rc, rs = V("ps", BANK * bank, BANK * bank + rb - ra), V(l, la, la + 128), V(l + "s", la, la + 128), V(r, ra, rb), V(r + "s", ra, rb)
         op("t", lambda q: q.matmul_mx(ap(out), ap(lc), ap(ls), ap(rc), ap(rs), True, True), [out], [lc, ls, rc, rs])
 
-    def pick(oc, os, wc, ws, lst):
-        op("v", lambda q: q.tensor_copy(ap(oc).bitcast(dt.uint32), ap(wc).bitcast(dt.uint32).indirect(ap(lst))), [oc], [wc, lst])
-        op("s", lambda q: q.activation(ap(os), ap(ws).indirect(ap(lst)), ACT.Copy), [os], [ws, lst])
+    def pick(o, w, lst):
+        op("v", lambda q: q.tensor_copy(ap(o).bitcast(dt.uint32), ap(w).bitcast(dt.uint32).indirect(ap(lst))), [o], [w, lst])
 
-    def load(q, sem, out, src):
-        op(q, lambda e: e.dma_start(ap(out), src), [out], [], dma=sem)
+    def dma(q, sem, dst, src, outs, ins):
+        op(q, lambda e: e.dma_start(dst, src), outs, ins, dma=sem)
 
-    def move(q, sem, out, in_, codes):
-        f = by if codes else ap
-        op(q, lambda e: e.dma_start(f(out), f(in_)), [out], [in_], dma=sem)
+    def move(sems, dst, da, src, sa, n):
+        for sem, x, f in ((sems, "", by), (sems + "s", "s", ap)):
+            o, i = V(dst + x, da, da + n), V(src + x, sa, sa + n)
+            dma("y", sem, f(o), f(i), [o], [i])
 
-    def store(q, sem, dst, in_, codes=False):
-        f = by if codes else ap
-        op(q, lambda e: e.dma_start(dst, f(in_)), [], [in_], dma=sem)
-
-    load("y", "dx", V("xt", 0, 512), T.x[:, :])
-    load("s", "drt", V("rtt"), T.rt[:, :])
-    load("y", "dw0", V("wt", 0, 1024), T.w[:, 0:1024])
-    load("s", "dw1", V("wt", 1024, 2048), T.w[:, 1024:2048])
-    load("y", "du", V("ut"), T.u[:, :])
-    load("y", "dv", V("vt"), T.v[:, :])
+    dma("y", "dx", ap(V("xt", 0, 512)), T.x[:, :], [V("xt", 0, 512)], [])
+    dma("s", "drt", ap(V("rtt")), T.rt[:, :], [V("rtt")], [])
+    dma("y", "dv", ap(V("vt")), T.v[:, :], [V("vt")], [])
+    dma("y", "dw0", ap(V("wt", 0, 1024)), T.w[:, 0:1024], [V("wt", 0, 1024)], [])
+    dma("s", "dw1", ap(V("wt", 1024, 2048)), T.w[:, 1024:2048], [V("wt", 1024, 2048)], [])
+    dma("y", "du", ap(V("ut")), T.u[:, :], [V("ut")], [])
 
     def iota(v, pattern, b):
         op("g", lambda q: q.iota(ap(v), pattern, b, 0, allow_small_or_imprecise_dtypes=True), [v], [])
@@ -249,100 +205,85 @@ def rank_program(g, core, T, topo):
     iota(V("ci", 64, 96), [[-1, 2], [0, 16]], 1)
     iota(V("ci", 96, 128), [[1, 2], [0, 16]], 0)
     iota(V("ci", 128, 160), [[0, 2], [1, 2], [0, 8]], 0)
+    iota(V("ci", 160, 192), [[0, 8], [64, 2], [0, 2]], 0)
     iota(V("bx"), [[0, 5], [1, 2], [0, 16]], 0)
     memset(V("xt", 512, 520), 0.0)
-    memset(V("zero"), 0.0)
-    memset(V("n4", 24, 32), 0.0)
-    memset(V("fr"), 8.0)
-    memset(V("qw", 0, Z0), -BIG)
-    memset(V("val", FW, TW), 0.0)
-    memset(V("lo"), 0.0)
-    memset(V("le"), 0.0)
-    memset(V("wn4"), 0.0)
-    memset(V("ones"), 1.0)
+    for v, x in ((V("zero"), 0.0), (V("n4", 24, 32), 0.0), (V("fr"), 8.0), (V("qw", 0, Z0), -BIG), (V("yw", 0, Z0), 0.0),
+                 (V("val", FW, TW), 0.0), (V("lo"), 0.0), (V("le"), 0.0), (V("wn4"), 0.0), (V("ones"), 1.0)):
+        memset(v, x)
     turn(V("cc"), V("ci"))
     kcol = V("cc", 0, 1, 0, 32)
-    ecol, even, odd, hcol = V("cc", 32, 33), V("cc", 64, 65), V("cc", 96, 97), V("cc", 128, 129)
+    ecol, even, odd, hcol, bcol = V("cc", 32, 33), V("cc", 64, 65), V("cc", 96, 97), V("cc", 128, 129), V("cc", 160, 161)
     ts(V("pm"), V("bx"), hcol, OP.is_equal)
+    ts(V("sc"), bcol, -1.0 / 128, OP.mult, 1.0, OP.add)
 
-    quant(V("rq"), V("rs"), V("rtt"))
-    quant(V("xq"), V("xs"), V("xt"))
-    mm(0, 128, V("xq", 0, 128), V("xs", 0, 128), V("rq"), V("rs"))
+    quant("rq", "rtt")
+    quant("xq", "xt")
+    mm(0, "xq", 0, "rq", 0, 128)
+    quant("vq", "vt")
     for e in (4, 5, 6, 7, 0, 1, 2, 3):
-        sc = V("ps", e, e + 1)
+        own = V("ps", e, e + 1)
         if e:
-            ts(V("cmp", 8 * e, 8 * e + e), V("ps", 0, e), sc, OP.is_ge)
-        ts(V("cmp", 9 * e, 8 * e + 8), V("ps", e, 8), sc, OP.is_gt)
+            ts(V("cmp", 8 * e, 9 * e), V("ps", 0, e), own, OP.is_ge)
+        ts(V("cmp", 9 * e, 8 * e + 8), V("ps", e, 8), own, OP.is_gt)
     for e in range(8):
-        i = EXP.index(e)
-        total(V("r8", i, i + 1), V("cmp", 8 * e, 8 * e + 8), "v" if e < 4 else "s", V("junk", 8 * (e % 4), 8 * (e % 4) + 8))
+        total(V("r8", e, e + 1), V("cmp", 8 * e, 8 * e + 8), "v" if e < 4 else "s", 8 * (e % 4))
     for k in range(3):
         ts(V("n4", k, 24, st=3), V("r8"), 1.0, OP.is_le)
     for a in range(4):
         turn(V("f0", 32 * a, 32 * a + 32), V("n4", 0, 32, 32 * a, 32 * a + 32))
-    scan(V("cb"), V("f0"), V("zero", 0, 128, 0, 32), kcol)
-    for m in range(NV, 16):
-        j = V("tms", 128 * (m - NV), 128 * (m - NV) + 128)
-        acc = V("lsc", m, m + 1)
-        bias = m + 0.5
-        op("s", lambda q: q.activation(ap(j), ap(V("cb")), ACT.Sign, bias=bias, scale=-1.0, accum_out=ap(acc)), [j, acc], [V("cb")])
-    for m in range(NV):
+    c0 = V("cb", 0, 128, 0, 32)
+    scan(c0, V("f0"), V("zero", 0, 128, 0, 32), kcol)
+    act(V("cb", 0, 128, 96, 128), c0, ACT.Identity, bias=-12.0)
+    for a in (1, 2):
+        ts(V("cb", 0, 128, 32 * a, 32 * a + 32), c0, 4.0 * a, OP.subtract)
+    for m in (2, 3):
+        act(V("tms", 128 * (m - 2), 128 * (m - 2) + 128), V("cb"), ACT.Sign, acc=V("lc", m, m + 1), bias=m + 0.5, scale=-1.0)
+    for m in (0, 1):
         ts(V("tmp", 128 * m, 128 * m + 128), V("cb"), float(m), OP.is_le)
-    for m in range(NV):
-        total(V("lt", m, m + 1), V("tmp", 128 * m, 128 * m + 128))
-    copy(V("lt", 16, 16 + NV), V("lt", 0, NV))
-    ts(V("lt", NV, 16), V("lsc", NV, 16), 0.5, OP.mult, 64.0, OP.add)
-    ts(V("lt", 16 + NV, 32), V("lsc", NV, 16), 0.5, OP.mult, 64.0, OP.add)
+    for m in (0, 1):
+        total(V("lc", m, m + 1), V("tmp", 128 * m, 128 * m + 128))
+    for a in range(4):
+        for d in (0, 16):
+            copy(V("lt", d + 4 * a, d + 4 * a + 4), V("lc", 0, 4, 32 * a, 32 * a + 32), "s" if d else "v")
     for a in range(4):
         turn(V("of", 0, 32, 32 * a, 32 * a + 32), V("lt"))
-    copy(V("off"), V("of", 0, 24))
+    ts(V("off"), V("of", 0, 24), V("sc"), OP.mult, bcol, OP.add)
 
-    def engines_of(n):
-        k = len(away) // n
-        return [sum(1 << x for x in away[k * i:k * i + k]) for i in range(n)], k
+    def ship(h, src, dst, sem, at):
+        to = [r for r in batch[h] if r != rank]
+        far = [r for r in to if chip[r] != topo.chip(core)]
+        k = len(away) // len(far)
+        d0 = at + CAPP * rank
+        for x, f in (("", by), ("s", ap)):
+            trs, ins, ls = [], [], 0
+            for r in to:
+                eng = near if r not in far else away[k * far.index(r):k * far.index(r) + k]
+                rid, pid, _s = topo.addr(T.cores[r])
+                s, d = V(src + x, CAPP * r, CAPP * r + CAPP), V(dst + x, d0, d0 + CAPP)
+                trs.append(RemoteDMATransfer(dst_ids=[DstId(rid=rid, pnc=pid)], dma_engine_mask=bits(eng), remote_sem=T.sem[sem],
+                                             src=f(s), dst=f(d)))
+                ins.append(s)
+                ls += len(eng)
+            send(lambda q: q.remote_dma_fused(trs, local_sem=T.sem["ls"]), ins, ls)
 
-    def ship(order, half, src, dst, sem, col_of, width, codes, off0=0, soff0=0):
-        f = by if codes else ap
-        to = [(i, T.cores[order[i]]) for i in range(4 * half, 4 * half + 4) if order[i] != rank]
-        far = [x for x in to if topo.chip(x[1]) != topo.chip(core)]
-        masks, k = engines_of(len(far))
-        trs, ins, ls = [], [], 0
-        for i, c in to:
-            if (i, c) in far:
-                mask, n = masks[far.index((i, c))], k
-            else:
-                mask, n = sum(1 << x for x in near), len(near)
-            rid, pid, _s = topo.addr(c)
-            s = V(src, soff0 + CAPP * i, soff0 + CAPP * i + CAPP)
-            at = off0 + CAPP * col_of(T.rank_of(c))
-            d = V(dst, at, at + CAPP)
-            trs.append(RemoteDMATransfer(dst_ids=[DstId(rid=rid, pnc=pid)], dma_engine_mask=mask, remote_sem=T.sem[sem],
-                                         src=f(s), dst=f(d)))
-            ins.append(s)
-            ls += n
-        send(lambda q: q.remote_dma_fused(trs, local_sem=T.sem["ls"]), ins, ls)
-
-    def landed(half):
-        far = 2 if half == 0 else 4
-        return 2 * (far * (len(away) // far) + (len(near) if half == 0 else 0))
+    def land(h, dst, sem, at):
+        others = [r for r in batch[h] if r != rank]
+        far = [r for r in others if chip[r] != topo.chip(core)]
+        n = 2 * (len(far) * (len(away) // len(far)) + len(near) * (len(others) - len(far)))
+        arrive(sem, n, [V(dst + x, at + CAPP * r, at + CAPP * r + CAPP) for r in others for x in ("", "s")])
 
     for h in range(2):
-        a, b = HALF * h, HALF * h + HALF
-        pick(V("xd", a, b), V("xds", a, b), V("xq"), V("xs"), V("off", 12 * h, 12 * h + 12))
-        ship(EXP, h, "xd", "xr", "xa%d" % (h + 1), lambda r: sources(r).index(rank), CAPP, True)
-        ship(EXP, h, "xds", "xrs", "xa%d" % (h + 1), lambda r: sources(r).index(rank), CAPP, False)
+        a = CAPP * batch[h][0]
+        lst = V("off", a // 16, a // 16 + 12)
+        pick(V("xd", a, a + HALF), V("xq"), lst)
+        act(V("xds", a, a + HALF), V("xqs"), ACT.Copy, lst)
+        ship(h, "xd", "xr", "xa%d" % h, 0)
         if h == 0:
-            m, n = CAPP * mine, CAPP * mine_src
-            move("y", "dxo", V("xr", n, n + CAPP), V("xd", m, m + CAPP), True)
-            move("y", "dxos", V("xrs", n, n + CAPP), V("xds", m, m + CAPP), False)
-            move("y", "dz", V("hr", 0, 2), V("xq", 128, 130), True)
-            move("y", "dzs", V("hrs", 0, 2), V("xs", 128, 130), False)
-    for h in range(2):
-        for i in range(4 * h, 4 * h + 4):
-            if SRC[i] != rank:
-                arrive("xa%d" % (h + 1), 0, [V("xr", CAPP * i, CAPP * i + CAPP), V("xrs", CAPP * i, CAPP * i + CAPP)])
+            move("dxo", "xr", CAPP * rank, "xd", CAPP * rank, CAPP)
+            move("dz", "hr", 0, "xq", 128, 2)
 
-    quant(V("wq"), V("ws"), V("wt"))
+    quant("wq", "wt")
     for j in range(4):
         copy(V("tr", 8 * j, 8 * j + 8), V("r8"), "s")
     for a in range(4):
@@ -350,96 +291,86 @@ def rank_program(g, core, T, topo):
     for a in range(4):
         copy(V("rk", 0, TW, 32 * a, 32 * a + 32), V("fr", 32, 192), "s")
         copy(V("rk", 0, TW, 32 * a, 32 * a + 16), V("fr", 16, 176, 0, 16), "s")
+    for t in range(4):
+        ts(V("ur", t, 512, st=4), V("ones"), V("ut", t, t + 1), OP.mult)
+    quant("uq", "ur")
     ts(V("nm"), V("rk"), 1.0, OP.is_le)
     ts(V("rk1"), V("rk"), 1.0, OP.add)
     scan(V("ct"), V("nm"), V("zero"), 0.0)
     ts(V("tk"), V("ct"), float(CAPP), OP.is_le)
-    ts(V("p1"), V("ct"), ecol, OP.add, 2.0, OP.mult)
+    ts(V("p1"), V("ct"), ecol, OP.add)
     tt(V("tk2"), V("tk"), V("nm"), OP.mult)
     tt(V("p2"), V("p1"), V("pm"), OP.mult)
     tt(V("t2"), V("tk2"), V("rk1"), OP.mult)
-    ts(V("role"), V("t2"), 1.0, OP.subtract)
 
     for h in range(2):
-        a, b = HALF * h, HALF * h + HALF
-        arrive("xa%d" % (h + 1), landed(h), [V("xr", c, c + CAPP) for c in range(a, b, CAPP) if c != CAPP * mine_src]
-               + [V("xrs", c, c + CAPP) for c in range(a, b, CAPP) if c != CAPP * mine_src])
+        a = CAPP * batch[h][0]
+        b = a + HALF
+        land(h, "xr", "xa%d" % h, 0)
         for i in (0, 2, 1, 3):
-            w = V("wq", 128 * i, 128 * i + 128), V("ws", 128 * i, 128 * i + 128)
-            mm(BANK * (4 * h + i), HALF, w[0], w[1], V("xr", a, b), V("xrs", a, b))
+            mm(4 * h + i, "wq", 128 * i, "xr", a, b)
         for i in range(4):
             r, o = V("ps", BANK * (4 * h + i), BANK * (4 * h + i) + HALF), V("ht", 4 * a + i, 4 * b, st=4)
             if i < 2:
                 ts(o, r, 0.0, OP.max, 0.0625, OP.mult)
             else:
-                op("s", lambda q: q.activation(ap(o), ap(r), ACT.Relu, scale=0.0625), [o], [r])
-        quant(V("hq", a, b), V("hs", a, b), V("ht", 4 * a, 4 * b))
-        ship(SRC, h, "hq", "hr", "ha%d" % (h + 1), lambda r: experts(r).index(rank), CAPP, True, Z0)
-        ship(SRC, h, "hs", "hrs", "ha%d" % (h + 1), lambda r: experts(r).index(rank), CAPP, False, Z0)
+                act(o, r, ACT.Relu, scale=0.0625)
+        quant("hq", "ht", a, b)
+        ship(h, "hq", "hr", "ha%d" % h, Z0)
         if h == 0:
-            n, m = CAPP * mine_src, Z0 + CAPP * mine
-            move("y", "dho", V("hr", m, m + CAPP), V("hq", n, n + CAPP), True)
-            move("y", "dhos", V("hrs", m, m + CAPP), V("hs", n, n + CAPP), False)
+            move("dho", "hr", Z0 + CAPP * rank, "hq", CAPP * rank, CAPP)
 
-    for t in range(4):
-        ts(V("ur", t, 512, st=4), V("ones"), V("ut", t, t + 1), OP.mult)
-    quant(V("uq"), V("us"), V("ur"))
-    quant(V("vq"), V("vs"), V("vt"))
-    ts(V("ma"), V("t2"), 1.0, OP.is_equal, 0.5, OP.mult)
-    ts(V("mb"), V("t2"), 2.0, OP.is_equal, 0.5, OP.mult)
+    ts(V("ma"), V("t2"), 1.0, OP.is_equal)
+    ts(V("mb"), V("t2"), 2.0, OP.is_equal)
     tt(V("va"), V("ma"), V("p2"), OP.mult)
     tt(V("vb"), V("mb"), V("p2"), OP.mult)
     turn(V("ta"), V("va"))
     turn(V("tb"), V("vb"))
     for k in range(8):
         total(V("la", k, k + 1), V("ta", 16 * k + 8, 16 * k + 24))
-        total(V("lb", k, k + 1), V("tb", 16 * k + 8, 16 * k + 24), "s", V("junk", 16 * (k % 2), 16 * (k % 2) + 16))
+        total(V("lb", k, k + 1), V("tb", 16 * k + 8, 16 * k + 24), "s", 32 + 16 * k)
     for j, l in ((0, "la"), (12, "lb")):
         ts(V("lo", j, j + 8), V(l), odd, OP.mult)
         ts(V("le", j + 1, j + 9), V(l), even, OP.mult)
     tt(V("lx"), V("lo"), V("le"), OP.add)
     copy(V("loff"), V("lx"))
+    ts(V("role"), V("t2"), 1.0, OP.subtract)
 
     for h in range(2):
-        a, b = Z0 + HALF * h, Z0 + HALF * h + HALF
-        skip = Z0 + CAPP * mine
-        arrive("ha%d" % (h + 1), landed(h), [V("hr", c, c + CAPP) for c in range(a, b, CAPP) if c != skip]
-               + [V("hrs", c, c + CAPP) for c in range(a, b, CAPP) if c != skip])
-        mm(BANK * h, HALF, V("uq"), V("us"), V("hr", a, b), V("hrs", a, b))
-        copy(V("qw", a, b), V("ps", BANK * h, BANK * h + HALF), "s" if h == 0 else "v")
-    lsta, lstb = V("loff", 0, 9), V("loff", 12, 21)
-    op("v", lambda q: q.tensor_copy(ap(V("ga")), ap(V("qw")).indirect(ap(lsta))), [V("ga")], [V("qw"), lsta])
-    op("s", lambda q: q.activation(ap(V("gb")), ap(V("qw")).indirect(ap(lstb)), ACT.Copy), [V("gb")], [V("qw"), lstb])
+        a = CAPP * batch[h][0]
+        wa, wb = Z0 + a, Z0 + a + HALF
+        land(h, "hr", "ha%d" % h, Z0)
+        mm(h, "uq", 0, "hr", wa, wb)
+        mm(2 + h, "vq", 0, "hr", wa, wb)
+        copy(V("qw", wa, wb), V("ps", BANK * h, BANK * h + HALF), "s" if h == 0 else "v")
+        if h == 1:
+            op("v", lambda q: q.tensor_copy(ap(V("ga")), ap(V("qw")).indirect(ap(V("loff", 0, 9)))), [V("ga")], [V("qw"), V("loff", 0, 9)])
+            act(V("gb"), V("qw"), ACT.Copy, V("loff", 12, 21))
+        copy(V("yw", wa, wb), V("ps", BANK * (2 + h), BANK * (2 + h) + HALF), "s")
     tt(V("dd"), V("gb"), V("ga"), OP.is_gt)
     tt(V("win"), V("dd"), V("role", 0, FW), OP.is_equal)
     scan(V("cw"), V("win"), V("zero", 0, FW), 0.0)
+    act(V("hf"), V("cw"), ACT.Sign, bias=CAPR + 0.5, scale=-1.0)
     tt(V("xp"), V("win"), V("p2", 0, FW), OP.mult)
-    ts(V("hf"), V("cw"), float(CAPR), OP.is_le, 0.5, OP.subtract)
     tt(V("val", 0, FW), V("xp"), V("hf"), OP.mult)
     turn(V("tv"), V("val"))
     for k in range(8):
-        total(V("s8", k, k + 1), V("tv", 16 * k + 8, 16 * k + 24), "v" if k < 5 else "s", V("junk", 16 * (k % 2), 16 * (k % 2) + 16))
+        total(V("s8", k, k + 1), V("tv", 16 * k + 8, 16 * k + 24), "v" if k < 5 else "s", 32 + 16 * k)
     copy(V("zoff"), V("s8"))
-    pick(V("zq"), V("zs"), V("hr"), V("hrs"), V("zoff"))
-    mm(BANK * 2, 128, V("vq"), V("vs"), V("zq"), V("zs"))
-    store("y", "doc", T.oc[:, :], V("zq"), True)
-    for k in range(4):
-        store("y", "dos%d" % k, T.osc[4 * k:4 * k + 4, :], V("zs", 0, 128, 32 * k, 32 * k + 4))
+    act(V("ysb"), V("yw"), ACT.Copy, V("zoff"))
+    dma("y", "dy", T.y[:, :], ap(V("ysb")), [], [V("ysb")])
     s = V("s8", 0, 8, 0, 32)
-    op("s", lambda q: q.activation(ap(V("wa")), ap(s), ACT.Abs), [V("wa")], [s])
-    ts(V("wh"), s, 1.0, OP.is_ge)
-    ts(V("wz"), s, 0.0, OP.is_equal, float(base - 100), OP.mult)
-    ts(V("wg"), V("wh"), 2.0, OP.mult, 1.0, OP.subtract)
-    ts(V("wk"), V("wh"), 1.0, OP.subtract)
-    mid = Z0 + (CAPP - 1) / 2.0
-    ts(V("we"), V("wa"), 1.0 / CAPP, OP.mult, base - mid / CAPP, OP.add)
-    tt(V("wj"), V("wz"), V("wk"), OP.add)
-    ts(V("ww"), V("we"), float(N), OP.is_ge, -float(N), OP.mult)
-    tt(V("wf"), V("we"), V("ww"), OP.add)
-    tt(V("wm"), V("wf"), V("wg"), OP.mult)
-    tt(V("wn4", 0, 8), V("wm"), V("wj"), OP.add)
+    mid = (Z0 + (CAPP - 1) / 2.0) / CAPP
+    ts(V("wa"), s, 1.0 / CAPP, OP.mult, mid - 1.0, OP.add)
+    ts(V("wh"), s, 1.0, OP.is_ge, 1.0 - 2.0 * mid, OP.mult)
+    ts(V("wz"), s, 0.0, OP.is_equal, -100.0, OP.mult)
+    tt(V("we"), V("wa"), V("wh"), OP.add)
+    tt(V("wn4", 0, 8), V("we"), V("wz"), OP.add)
     turn(V("wnt"), V("wn4"))
-    copy(V("ysb"), V("ps", BANK * 2, BANK * 2 + 128), "s")
-    store("s", "dy", T.y[:, :], V("ysb"))
-    store("y", "dwn", T.wn[:, :], V("wnt", 0, 16, 0, 8))
+    dma("y", "dwn", T.wn[:, :], ap(V("wnt", 0, 16, 0, 8)), [], [V("wnt", 0, 16, 0, 8)])
+    pick(V("zq"), V("hr"), V("zoff"))
+    act(V("zqs"), V("hrs"), ACT.Copy, V("zoff"))
+    dma("y", "doc", T.oc[:, :], by(V("zq")), [], [V("zq")])
+    for k in range(4):
+        dma("s", "dos%d" % k, T.osc[4 * k:4 * k + 4, :], ap(V("zqs", 0, 128, 32 * k, 32 * k + 4)), [], [V("zqs")])
     finish()

@@ -3,36 +3,38 @@ from concourse.mybir import dt, AluOpType, AxisListType, ActivationFunctionType
 
 OP, ACT = AluOpType, ActivationFunctionType
 CAPP, CAPR = 48, 32
-HALF = 4 * CAPP
+LEAST = 128
 Z0 = 32
+END = Z0 + 8 * CAPP
+FULL = END + Z0
 FW = 144
 TW = 160
 BIG = 9e29
 BANK = 512
 
-SCRATCH = {"ps": ("psum", [128, 8 * BANK], "float32"), "we": ("sbuf", [32, 8], "int32"), "f0": ("sbuf", [32, 128], "float32"),
+SCRATCH = {"ps": ("psum", [128, 8 * BANK], "float32"), "we": ("sbuf", [32, 8], "int32"), "f0": ("sbuf", [32, 128], "bfloat16"),
+           "zb": ("sbuf", [32, 128], "bfloat16"), "n4": ("sbuf", [128, 32], "bfloat16"),
            "lt": ("sbuf", [32, 32], "float32"), "fr": ("sbuf", [32, 192], "float32"), "wn4": ("sbuf", [32, 32], "float32"),
            "wnt": ("sbuf", [32, 32], "float32"), "wa": ("sbuf", [32, 8], "float32"), "wh": ("sbuf", [32, 8], "float32"),
-           "wz": ("sbuf", [32, 8], "float32"), "off": ("sbuf", [128, 24], "uint16"), "loff": ("sbuf", [128, 24], "uint16"),
-           "zoff": ("sbuf", [128, 8], "uint16")}
-for _n, _w in (("xt", 520), ("rtt", 512), ("wt", 2048), ("ut", 512), ("ur", 512), ("vt", 512), ("ones", 128), ("ht", 1536),
-               ("cb", 128), ("tmp", 256), ("tms", 256)):
+           "wz": ("sbuf", [32, 8], "float32"), "off": ("sbuf", [128, 24], "uint16"), "loff": ("sbuf", [128, 32], "uint16"),
+           "zoff": ("sbuf", [128, 8], "uint16"), "aboff": ("sbuf", [128, 8], "uint16"), "soff": ("sbuf", [128, 2], "uint16")}
+for _n, _w in (("xt", 512 + 4 * Z0), ("rtt", 512), ("wt", 2048), ("ut", 512), ("ur", 512), ("vt", 512), ("ones", 128),
+               ("ht", 4 * FULL), ("cb", 128), ("tmp", 128), ("tms", 384)):
     SCRATCH[_n] = ("sbuf", [128, _w], "bfloat16")
-for _n, _w in (("xq", 130), ("rq", 128), ("wq", 512), ("uq", 128), ("vq", 128), ("xd", 384), ("xr", 384), ("hq", 384),
-               ("hr", 416), ("zq", 128)):
+for _n, _w in (("xq", 128 + Z0), ("rq", 128), ("rp", 128), ("wq", 512), ("uq", 128), ("vq", 128), ("xd", 384), ("xr", FULL),
+               ("hq0", 192), ("hq1", 128), ("hq2", 128), ("hr", FULL), ("zq", 128)):
     SCRATCH[_n] = ("sbuf", [128, _w], "float8_e4m3fn_x4")
     SCRATCH[_n + "s"] = ("sbuf", [128, _w], "uint8")
-for _n, _w in (("ci", 192), ("cc", 192), ("sc", 1), ("bx", TW), ("pm", TW), ("zero", TW),
-               ("cmp", 64), ("junk", 160), ("r8", 8), ("n4", 32), ("lc", 4), ("of", 32),
-               ("tr", 32), ("rk", TW), ("nm", TW), ("ct", TW), ("tk", TW), ("tk2", TW), ("rk1", TW), ("t2", TW), ("role", TW),
-               ("p1", TW), ("p2", TW), ("ma", TW), ("mb", TW), ("va", TW), ("vb", TW), ("ta", TW), ("tb", TW),
-               ("la", 8), ("lb", 8), ("lo", 24), ("le", 24), ("lx", 24),
-               ("qw", 416), ("yw", 416), ("ga", FW), ("gb", FW), ("dd", FW), ("win", FW), ("cw", FW), ("hf", FW), ("xp", FW),
-               ("val", TW), ("tv", TW), ("s8", 8), ("ysb", 128)):
+for _n, _w in (("ci", 224), ("cc", 224), ("c2", 4), ("bc", 1), ("sc", 1), ("bx", TW), ("pm", TW), ("zero", TW), ("d0", 64),
+               ("thr", 8), ("c8", 8), ("seg", 128), ("bs", 64), ("cp", 64), ("sg", 64), ("r8", 8), ("lc", 4), ("of", 32),
+               ("tr", 32), ("rk", TW), ("nm", TW), ("ct", TW), ("ov", TW), ("role", TW),
+               ("p1", TW), ("p2", TW), ("ma", TW), ("mb", TW), ("va", TW), ("vb", TW), ("ta", TW), ("tb", TW), ("lab", 256),
+               ("qw", END), ("yw", END), ("ga", FW), ("gb", FW), ("dd", FW), ("win", FW), ("cw", FW), ("hf", FW), ("xp", FW),
+               ("val", TW), ("tv", TW), ("s8", 128), ("ysb", 128)):
     SCRATCH[_n] = ("sbuf", [128, _w], "float32")
-DMAS = ["dx", "drt", "dw0", "dw1", "du", "dv", "dxo", "dxos", "dz", "dzs", "dho", "dhos", "doc", "dos0", "dos1", "dos2",
-        "dos3", "dy", "dwn"]
-SEMAPHORES = ["cv", "cs", "ct", "cg", "ls", "xa0", "xa1", "ha0", "ha1"] + DMAS
+DMAS = ["dx", "drt", "dw0", "dw1", "du", "dv", "dxo", "dxos", "dzx", "dzxs", "dz", "dzs", "dze", "dzes", "dho", "dhos",
+        "doc", "dos0", "dos1", "dos2", "dos3", "dy", "dwn"]
+SEMAPHORES = ["cv", "cs", "ct", "cg", "ls", "xa0", "xa1", "xa2", "ha0", "ha1", "ha2"] + DMAS
 
 
 def _runner(g, T):
@@ -111,11 +113,17 @@ def rank_program(g, core, T, topo):
     N = len(T.cores)
 
     chip = [topo.chip(c) for c in T.cores]
-    first = rank // 4
-    batch = [[4 * (first ^ h) + i for i in range(4)] for h in range(2)]
+    first, half = rank // 4, rank % 4 // 2
+    other = 4 * (1 - first)
+    batch = []
+    for r0, n in ((4 * first, 4), (other + 2 * half, 2), (other + 2 * (1 - half), 2)):
+        c0, c1 = Z0 + CAPP * r0, Z0 + CAPP * (r0 + n)
+        more = max(LEAST - (c1 - c0), 0)
+        w0, w1 = (c0 - more, c1) if r0 % 4 == 0 else (c0, c1 + more)
+        batch.append((list(range(r0, r0 + n)), c0, c1, w0, w1))
     away = topo.engines(core, next(c for c in T.cores if topo.chip(c) != topo.chip(core)))
     peer = next(c for c in T.cores if topo.chip(c) == topo.chip(core) and c != core)
-    near = [e for e in topo.engines(core, peer) if e not in away][:2]
+    near = [e for e in topo.engines(core, peer) if e not in away][:len(away) // 2]
 
     def bits(es):
         return sum(1 << e for e in es)
@@ -136,14 +144,23 @@ def rank_program(g, core, T, topo):
 
     def act(out, in_, f, lst=None, acc=None, **k):
         src = ap(in_) if lst is None else ap(in_).indirect(ap(lst))
-        kk = dict(k) if acc is None else dict(k, accum_out=ap(acc))
-        op("s", lambda q: q.activation(ap(out), src, f, **kk), [out] + ([acc] if acc else []), [in_] + ([lst] if lst else []))
+        cols = [x for x in k.values() if isinstance(x, tuple)]
+        kk = {n: ap(x) if isinstance(x, tuple) else x for n, x in k.items()}
+        if acc is not None:
+            kk["accum_out"] = ap(acc)
+        op("s", lambda q: q.activation(ap(out), src, f, **kk), [out] + ([acc] if acc else []),
+           [in_] + cols + ([lst] if lst else []))
 
-    def copy(out, in_, q="v"):
+    def fill(v, x):
+        n = len(range(v[3], v[4], v[5]))
+        act(v, V("zero", 0, n, v[1], v[2]), ACT.Identity, bias=x)
+
+    def copy(out, in_, q="v", lst=None):
         if q == "v":
-            op("v", lambda e: e.tensor_copy(ap(out), ap(in_)), [out], [in_])
+            src = ap(in_) if lst is None else ap(in_).indirect(ap(lst))
+            op("v", lambda e: e.tensor_copy(ap(out), src), [out], [in_] + ([lst] if lst else []))
         else:
-            act(out, in_, ACT.Copy)
+            act(out, in_, ACT.Copy, lst)
 
     def tt(out, a, b, o):
         op("v", lambda q: q.tensor_tensor(ap(out), ap(a), ap(b), o), [out], [a, b])
@@ -156,11 +173,11 @@ def rank_program(g, core, T, topo):
         else:
             op("v", lambda q: q.tensor_scalar(ap(out), ap(a), x1, x2, o1, o2), [out], ins)
 
-    def total(out, in_, q="v", at=0):
-        if q == "v":
-            op("v", lambda e: e.tensor_reduce(ap(out), ap(in_), AxisListType.X, OP.add), [out], [in_])
-        else:
-            act(V("junk", at, at + in_[4] - in_[3]), in_, ACT.Identity, acc=out)
+    def total(out, in_):
+        op("v", lambda e: e.tensor_reduce(ap(out), ap(in_), AxisListType.X, OP.add), [out], [in_])
+
+    def runs(out, mask, in_):
+        op("v", lambda q: q.tensor_tensor_scan(ap(out), ap(mask), ap(in_), 0.0, OP.mult, OP.add), [out], [mask, in_])
 
     def scan(out, a, b, init):
         ini = ap(init) if isinstance(init, tuple) else init
@@ -171,7 +188,8 @@ def rank_program(g, core, T, topo):
         op("v", lambda q: q.transpose(ap(out), ap(in_)), [out], [in_])
 
     def quant(c, t, a=0, b=None):
-        o, s, i = V(c, a, b), V(c + "s", a, b), V(t, 4 * a, None if b is None else 4 * b)
+        n = SCRATCH[t][1][1] // 4 if b is None else b - a
+        o, s, i = V(c, 0, n), V(c + "s", 0, n), V(t, 4 * a, 4 * (a + n))
         op("v", lambda q: q.quantize_mx(ap(o), ap(s), ap(i)), [o, s], [i])
 
     def mm(bank, l, la, r, ra, rb):
@@ -189,164 +207,183 @@ def rank_program(g, core, T, topo):
             o, i = V(dst + x, da, da + n), V(src + x, sa, sa + n)
             dma("y", sem, f(o), f(i), [o], [i])
 
+    dma("s", "drt", ap(V("rtt", 0, 4 * N)), T.rt[:, 0:4 * N], [V("rtt", 0, 4 * N)], [])
     dma("y", "dx", ap(V("xt", 0, 512)), T.x[:, :], [V("xt", 0, 512)], [])
-    dma("s", "drt", ap(V("rtt")), T.rt[:, :], [V("rtt")], [])
     dma("y", "dv", ap(V("vt")), T.v[:, :], [V("vt")], [])
     dma("y", "dw0", ap(V("wt", 0, 1024)), T.w[:, 0:1024], [V("wt", 0, 1024)], [])
-    dma("s", "dw1", ap(V("wt", 1024, 2048)), T.w[:, 1024:2048], [V("wt", 1024, 2048)], [])
+    dma("y", "dw1", ap(V("wt", 1024, 2048)), T.w[:, 1024:2048], [V("wt", 1024, 2048)], [])
     dma("y", "du", ap(V("ut")), T.u[:, :], [V("ut")], [])
 
-    def iota(v, pattern, b):
-        op("g", lambda q: q.iota(ap(v), pattern, b, 0, allow_small_or_imprecise_dtypes=True), [v], [])
+    def iota(v, pattern, b, cm=0):
+        op("g", lambda q: q.iota(ap(v), pattern, b, cm, allow_small_or_imprecise_dtypes=True), [v], [])
 
-    iota(V("ci", 0, 24), [[0, 8], [-16, 3]], 0)
-    iota(V("ci", 24, 32), [[0, 8]], 0)
-    iota(V("ci", 32, 64), [[0, 4], [CAPP, 8]], Z0 - 1)
-    iota(V("ci", 64, 96), [[-1, 2], [0, 16]], 1)
-    iota(V("ci", 96, 128), [[1, 2], [0, 16]], 0)
-    iota(V("ci", 128, 160), [[0, 2], [1, 2], [0, 8]], 0)
-    iota(V("ci", 160, 192), [[0, 8], [64, 2], [0, 2]], 0)
+    iota(V("ci", 0, 32), [[0, 4], [1, 8]], 0)
+    iota(V("ci", 32, 64), [[0, 2], [1, 2], [0, 8]], 0)
+    iota(V("c2"), [[2, 4]], 0)
+    iota(V("ci", 64, 88), [[0, 8], [-16, 3]], 0, -4)
+    iota(V("ci", 88, 96), [[0, 8]], 0)
+    iota(V("ci", 96, 128), [[0, 8], [1, 4]], 0)
+    iota(V("thr"), [[-1, 8]], 7)
+    iota(V("c8"), [[-1, 8]], 8)
+    iota(V("ci", 128, 160), [[0, 4], [CAPP, 8]], Z0 - 1)
+    iota(V("ci", 160, 192), [[0, 2], [1, 2], [0, 8]], -1)
+    iota(V("ci", 192, 224), [[16, 2], [16, 16]], -1)
     iota(V("bx"), [[0, 5], [1, 2], [0, 16]], 0)
-    memset(V("xt", 512, 520), 0.0)
-    for v, x in ((V("zero"), 0.0), (V("n4", 24, 32), 0.0), (V("fr"), 8.0), (V("qw", 0, Z0), -BIG), (V("yw", 0, Z0), 0.0),
-                 (V("val", FW, TW), 0.0), (V("lo"), 0.0), (V("le"), 0.0), (V("wn4"), 0.0), (V("ones"), 1.0)):
-        memset(v, x)
-    turn(V("cc"), V("ci"))
-    kcol = V("cc", 0, 1, 0, 32)
-    ecol, even, odd, hcol, bcol = V("cc", 32, 33), V("cc", 64, 65), V("cc", 96, 97), V("cc", 128, 129), V("cc", 160, 161)
-    ts(V("pm"), V("bx"), hcol, OP.is_equal)
-    ts(V("sc"), bcol, -1.0 / 128, OP.mult, 1.0, OP.add)
+    ecol, hcol, mcol, pcol, gcol, lcol = (V("cc", c, c + 1) for c in (0, 32, 96, 128, 160, 192))
+    memset(V("rtt", 4 * N, 512), 0.0)
+    memset(V("zero"), 0.0)
+    memset(V("d0"), 1.0)
+    turn(V("cc", 0, 64), V("ci", 0, 64))
+    memset(V("zb"), 0.0)
+    memset(V("d0", 9, 64, st=9), -1.0)
+    memset(V("xt", 512, 512 + 4 * Z0), 0.0)
+    ts(V("aboff", 0, 4), V("c2"), hcol, OP.add, ecol, OP.min)
+    ts(V("aboff", 4, 8), V("c2"), hcol, OP.add, ecol, OP.max)
+    memset(V("d0", 0, 64, st=8), 0.0)
+    turn(V("cc", 64, 128), V("ci", 64, 128))
+    fill(V("n4", 24, 32), 0.0)
+    for c0 in (0, 160):
+        fill(V("fr", c0, c0 + 32), 8.0)
+    fill(V("qw", 0, Z0), -BIG)
+    fill(V("yw", 0, Z0), 0.0)
 
     quant("rq", "rtt")
+    pick(V("rp"), V("rq"), V("aboff"))
+    act(V("rps"), V("rqs"), ACT.Copy, V("aboff"))
     quant("xq", "xt")
-    mm(0, "xq", 0, "rq", 0, 128)
-    quant("vq", "vt")
-    for e in (4, 5, 6, 7, 0, 1, 2, 3):
-        own = V("ps", e, e + 1)
-        if e:
-            ts(V("cmp", 8 * e, 9 * e), V("ps", 0, e), own, OP.is_ge)
-        ts(V("cmp", 9 * e, 8 * e + 8), V("ps", e, 8), own, OP.is_gt)
-    for e in range(8):
-        total(V("r8", e, e + 1), V("cmp", 8 * e, 8 * e + 8), "v" if e < 4 else "s", 8 * (e % 4))
+    mm(0, "xq", 0, "rp", 0, 128)
+    ts(V("bc"), mcol, 0.5, OP.is_ge, 64.0, OP.mult)
+    copy(V("bs"), V("ps", 64, 128))
+    tt(V("cp"), V("ps", 0, 64), V("bs"), OP.is_ge)
+    runs(V("sg"), V("d0"), V("cp"))
+    rank8 = V("sg", 7, 64, st=8)
     for k in range(3):
-        ts(V("n4", k, 24, st=3), V("r8"), 1.0, OP.is_le)
+        tt(V("n4", k, 24, st=3), rank8, V("thr"), OP.is_ge)
+    tt(V("r8"), V("c8"), rank8, OP.subtract)
     for a in range(4):
         turn(V("f0", 32 * a, 32 * a + 32), V("n4", 0, 32, 32 * a, 32 * a + 32))
-    c0 = V("cb", 0, 128, 0, 32)
-    scan(c0, V("f0"), V("zero", 0, 128, 0, 32), kcol)
-    act(V("cb", 0, 128, 96, 128), c0, ACT.Identity, bias=-12.0)
-    for a in (1, 2):
-        ts(V("cb", 0, 128, 32 * a, 32 * a + 32), c0, 4.0 * a, OP.subtract)
-    for m in (2, 3):
-        act(V("tms", 128 * (m - 2), 128 * (m - 2) + 128), V("cb"), ACT.Sign, acc=V("lc", m, m + 1), bias=m + 0.5, scale=-1.0)
-    for m in (0, 1):
-        ts(V("tmp", 128 * m, 128 * m + 128), V("cb"), float(m), OP.is_le)
-    for m in (0, 1):
-        total(V("lc", m, m + 1), V("tmp", 128 * m, 128 * m + 128))
+    ts(V("sc"), V("bc"), -1.0 / 128, OP.mult, 1.0, OP.add)
+    for a in range(4):
+        scan(V("cb", 0, 128, 32 * a, 32 * a + 32), V("f0"), V("zb"), V("cc", 64 + a, 65 + a, 0, 32))
+    for j in range(4):
+        copy(V("tr", 8 * j, 8 * j + 8), V("r8"), "s")
+    for m in (1, 2, 3):
+        act(V("tms", 128 * (m - 1), 128 * m), V("cb"), ACT.Sign, acc=V("lc", m, m + 1), bias=m + 0.5, scale=-1.0)
+    ts(V("tmp"), V("cb"), 0.0, OP.is_le)
+    total(V("lc", 0, 1), V("tmp"))
     for a in range(4):
         for d in (0, 16):
             copy(V("lt", d + 4 * a, d + 4 * a + 4), V("lc", 0, 4, 32 * a, 32 * a + 32), "s" if d else "v")
     for a in range(4):
         turn(V("of", 0, 32, 32 * a, 32 * a + 32), V("lt"))
-    ts(V("off"), V("of", 0, 24), V("sc"), OP.mult, bcol, OP.add)
+    ts(V("off"), V("of", 0, 24), V("sc"), OP.mult, V("bc"), OP.add)
 
-    def ship(h, src, dst, sem, at):
-        to = [r for r in batch[h] if r != rank]
+    def parts(h):
+        to = [r for r in batch[h][0] if r != rank]
         far = [r for r in to if chip[r] != topo.chip(core)]
-        k = len(away) // len(far)
-        d0 = at + CAPP * rank
+        return to, far, len(away) // len(far)
+
+    def ship(h, src, s0, dst, sem):
+        to, far, k = parts(h)
+        d0 = Z0 + CAPP * rank
         for x, f in (("", by), ("s", ap)):
             trs, ins, ls = [], [], 0
             for r in to:
                 eng = near if r not in far else away[k * far.index(r):k * far.index(r) + k]
                 rid, pid, _s = topo.addr(T.cores[r])
-                s, d = V(src + x, CAPP * r, CAPP * r + CAPP), V(dst + x, d0, d0 + CAPP)
+                a = Z0 + CAPP * r - s0
+                s, d = V(src + x, a, a + CAPP), V(dst + x, d0, d0 + CAPP)
                 trs.append(RemoteDMATransfer(dst_ids=[DstId(rid=rid, pnc=pid)], dma_engine_mask=bits(eng), remote_sem=T.sem[sem],
                                              src=f(s), dst=f(d)))
                 ins.append(s)
                 ls += len(eng)
             send(lambda q: q.remote_dma_fused(trs, local_sem=T.sem["ls"]), ins, ls)
 
-    def land(h, dst, sem, at):
-        others = [r for r in batch[h] if r != rank]
-        far = [r for r in others if chip[r] != topo.chip(core)]
-        n = 2 * (len(far) * (len(away) // len(far)) + len(near) * (len(others) - len(far)))
-        arrive(sem, n, [V(dst + x, at + CAPP * r, at + CAPP * r + CAPP) for r in others for x in ("", "s")])
+    def land(h, dst, sem):
+        to, far, k = parts(h)
+        n = 2 * (len(far) * k + len(near) * (len(to) - len(far)))
+        arrive(sem, n, [V(dst + x, Z0 + CAPP * r, Z0 + CAPP * r + CAPP) for r in to for x in ("", "s")])
 
-    for h in range(2):
-        a = CAPP * batch[h][0]
-        lst = V("off", a // 16, a // 16 + 12)
-        pick(V("xd", a, a + HALF), V("xq"), lst)
-        act(V("xds", a, a + HALF), V("xqs"), ACT.Copy, lst)
-        ship(h, "xd", "xr", "xa%d" % h, 0)
+    for h, (_rs, c0, c1, _w0, _w1) in enumerate(batch):
+        a, b = c0 - Z0, c1 - Z0
+        lst = V("off", a // 16, b // 16)
+        pick(V("xd", a, b), V("xq"), lst)
+        act(V("xds", a, b), V("xqs"), ACT.Copy, lst)
+        ship(h, "xd", Z0, "xr", "xa%d" % h)
         if h == 0:
-            move("dxo", "xr", CAPP * rank, "xd", CAPP * rank, CAPP)
-            move("dz", "hr", 0, "xq", 128, 2)
+            move("dxo", "xr", Z0 + CAPP * rank, "xd", CAPP * rank, CAPP)
+            move("dzx", "xr", END if first == 0 else 0, "xq", 128, Z0)
+            move("dz", "hr", 0, "xq", 128, Z0)
+            if first == 0:
+                move("dze", "hr", END, "xq", 128, Z0)
 
-    quant("wq", "wt")
-    for j in range(4):
-        copy(V("tr", 8 * j, 8 * j + 8), V("r8"), "s")
     for a in range(4):
         turn(V("fr", 32 + 32 * a, 64 + 32 * a), V("tr", 0, 32, 32 * a, 32 * a + 32))
-    for a in range(4):
-        copy(V("rk", 0, TW, 32 * a, 32 * a + 32), V("fr", 32, 192), "s")
-        copy(V("rk", 0, TW, 32 * a, 32 * a + 16), V("fr", 16, 176, 0, 16), "s")
+    memset(V("ones"), 1.0)
+    quant("wq", "wt")
     for t in range(4):
         ts(V("ur", t, 512, st=4), V("ones"), V("ut", t, t + 1), OP.mult)
-    quant("uq", "ur")
+    turn(V("cc", 128, 224), V("ci", 128, 224))
+    for a in range(4):
+        q = "v" if a == 3 else "s"
+        copy(V("rk", 0, TW, 32 * a, 32 * a + 32), V("fr", 32, 192), q)
+        if a == 3:
+            quant("uq", "ur")
+        copy(V("rk", 0, TW, 32 * a, 32 * a + 16), V("fr", 16, 176, 0, 16), q)
+    act(V("pm"), V("bx"), ACT.Abs, bias=gcol)
+    ts(V("soff", 0, 1), lcol, 0.0, OP.max, 255.0, OP.min)
+    ts(V("soff", 1, 2), lcol, 128.0, OP.add, 255.0, OP.min)
     ts(V("nm"), V("rk"), 1.0, OP.is_le)
-    ts(V("rk1"), V("rk"), 1.0, OP.add)
     scan(V("ct"), V("nm"), V("zero"), 0.0)
-    ts(V("tk"), V("ct"), float(CAPP), OP.is_le)
-    ts(V("p1"), V("ct"), ecol, OP.add)
-    tt(V("tk2"), V("tk"), V("nm"), OP.mult)
-    tt(V("p2"), V("p1"), V("pm"), OP.mult)
-    tt(V("t2"), V("tk2"), V("rk1"), OP.mult)
+    quant("vq", "vt")
+    act(V("ov"), V("ct"), ACT.Relu, scale=2.0, bias=-2.0 * CAPP)
+    ts(V("p1"), V("ct"), pcol, OP.add)
+    m0 = END if first == 0 else 0
+    fill(V("ht", 4 * m0, 4 * m0 + 4 * Z0), 0.0)
+    fill(V("val", FW, TW), 0.0)
+    fill(V("wn4"), 0.0)
+    fill(V("seg"), 1.0)
+    fill(V("seg", 0, 128, st=16), 0.0)
 
-    for h in range(2):
-        a = CAPP * batch[h][0]
-        b = a + HALF
-        land(h, "xr", "xa%d" % h, 0)
+    for h, (_rs, c0, c1, w0, w1) in enumerate(batch):
+        land(h, "xr", "xa%d" % h)
+        banks = [4 * (h % 2) + i for i in range(4)]
         for i in (0, 2, 1, 3):
-            mm(4 * h + i, "wq", 128 * i, "xr", a, b)
+            mm(banks[i], "wq", 128 * i, "xr", w0, w1)
         for i in range(4):
-            r, o = V("ps", BANK * (4 * h + i), BANK * (4 * h + i) + HALF), V("ht", 4 * a + i, 4 * b, st=4)
+            r, o = V("ps", BANK * banks[i] + c0 - w0, BANK * banks[i] + c1 - w0), V("ht", 4 * c0 + i, 4 * c1, st=4)
             if i < 2:
                 ts(o, r, 0.0, OP.max, 0.0625, OP.mult)
             else:
                 act(o, r, ACT.Relu, scale=0.0625)
-        quant("hq", "ht", a, b)
-        ship(h, "hq", "hr", "ha%d" % h, Z0)
+        hq = "hq%d" % h
+        quant(hq, "ht", w0, w1)
+        ship(h, hq, w0, "hr", "ha%d" % h)
         if h == 0:
-            move("dho", "hr", Z0 + CAPP * rank, "hq", CAPP * rank, CAPP)
+            move("dho", "hr", Z0 + CAPP * rank, hq, Z0 + CAPP * rank - w0, CAPP)
 
-    ts(V("ma"), V("t2"), 1.0, OP.is_equal)
-    ts(V("mb"), V("t2"), 2.0, OP.is_equal)
-    tt(V("va"), V("ma"), V("p2"), OP.mult)
+    tt(V("role"), V("rk"), V("ov"), OP.add)
+    tt(V("p2"), V("p1"), V("pm"), OP.mult)
+    act(V("ma"), V("role"), ACT.Relu, scale=-1.0, bias=1.0)
+    ts(V("mb"), V("role"), 1.0, OP.is_equal)
     tt(V("vb"), V("mb"), V("p2"), OP.mult)
-    turn(V("ta"), V("va"))
+    tt(V("va"), V("ma"), V("p2"), OP.mult)
     turn(V("tb"), V("vb"))
-    for k in range(8):
-        total(V("la", k, k + 1), V("ta", 16 * k + 8, 16 * k + 24))
-        total(V("lb", k, k + 1), V("tb", 16 * k + 8, 16 * k + 24), "s", 32 + 16 * k)
-    for j, l in ((0, "la"), (12, "lb")):
-        ts(V("lo", j, j + 8), V(l), odd, OP.mult)
-        ts(V("le", j + 1, j + 9), V(l), even, OP.mult)
-    tt(V("lx"), V("lo"), V("le"), OP.add)
-    copy(V("loff"), V("lx"))
-    ts(V("role"), V("t2"), 1.0, OP.subtract)
+    turn(V("ta"), V("va"))
+    runs(V("lab", 128, 256), V("seg"), V("tb", 8, 136))
+    runs(V("lab", 0, 128), V("seg"), V("ta", 8, 136))
+    copy(V("loff"), V("lab"), "v", V("soff"))
 
-    for h in range(2):
-        a = CAPP * batch[h][0]
-        wa, wb = Z0 + a, Z0 + a + HALF
-        land(h, "hr", "ha%d" % h, Z0)
-        mm(h, "uq", 0, "hr", wa, wb)
-        mm(2 + h, "vq", 0, "hr", wa, wb)
-        copy(V("qw", wa, wb), V("ps", BANK * h, BANK * h + HALF), "s" if h == 0 else "v")
-        if h == 1:
-            op("v", lambda q: q.tensor_copy(ap(V("ga")), ap(V("qw")).indirect(ap(V("loff", 0, 9)))), [V("ga")], [V("qw"), V("loff", 0, 9)])
-            act(V("gb"), V("qw"), ACT.Copy, V("loff", 12, 21))
-        copy(V("yw", wa, wb), V("ps", BANK * (2 + h), BANK * (2 + h) + HALF), "s")
+    last = len(batch) - 1
+    for h, (_rs, c0, c1, w0, w1) in enumerate(batch):
+        land(h, "hr", "ha%d" % h)
+        mm(h, "uq", 0, "hr", w0, w1)
+        mm(3 + h, "vq", 0, "hr", w0, w1)
+        copy(V("qw", c0, c1), V("ps", BANK * h + c0 - w0, BANK * h + c1 - w0), "v" if h == last else "s")
+        if h == last:
+            copy(V("ga"), V("qw"), "v", V("loff", 0, 9))
+            copy(V("gb"), V("qw"), "s", V("loff", 16, 25))
+        copy(V("yw", c0, c1), V("ps", BANK * (3 + h) + c0 - w0, BANK * (3 + h) + c1 - w0), "s")
     tt(V("dd"), V("gb"), V("ga"), OP.is_gt)
     tt(V("win"), V("dd"), V("role", 0, FW), OP.is_equal)
     scan(V("cw"), V("win"), V("zero", 0, FW), 0.0)
@@ -354,23 +391,22 @@ def rank_program(g, core, T, topo):
     tt(V("xp"), V("win"), V("p2", 0, FW), OP.mult)
     tt(V("val", 0, FW), V("xp"), V("hf"), OP.mult)
     turn(V("tv"), V("val"))
-    for k in range(8):
-        total(V("s8", k, k + 1), V("tv", 16 * k + 8, 16 * k + 24), "v" if k < 5 else "s", 32 + 16 * k)
-    copy(V("zoff"), V("s8"))
+    runs(V("s8"), V("seg"), V("tv", 8, 136))
+    copy(V("zoff"), V("s8", 15, 128, st=16))
     act(V("ysb"), V("yw"), ACT.Copy, V("zoff"))
     dma("y", "dy", T.y[:, :], ap(V("ysb")), [], [V("ysb")])
-    s = V("s8", 0, 8, 0, 32)
+    s = V("s8", 15, 128, 0, 32, 16)
     mid = (Z0 + (CAPP - 1) / 2.0) / CAPP
     ts(V("wa"), s, 1.0 / CAPP, OP.mult, mid - 1.0, OP.add)
     ts(V("wh"), s, 1.0, OP.is_ge, 1.0 - 2.0 * mid, OP.mult)
     ts(V("wz"), s, 0.0, OP.is_equal, -100.0, OP.mult)
+    pick(V("zq"), V("hr", 0, END), V("zoff"))
+    dma("y", "doc", T.oc[:, :], by(V("zq")), [], [V("zq")])
+    act(V("zqs"), V("hrs", 0, END), ACT.Copy, V("zoff"))
+    for k in range(4):
+        dma("s" if k < 2 else "y", "dos%d" % k, T.osc[4 * k:4 * k + 4, :], ap(V("zqs", 0, 128, 32 * k, 32 * k + 4)), [], [V("zqs")])
     tt(V("we"), V("wa"), V("wh"), OP.add)
     tt(V("wn4", 0, 8), V("we"), V("wz"), OP.add)
     turn(V("wnt"), V("wn4"))
-    dma("y", "dwn", T.wn[:, :], ap(V("wnt", 0, 16, 0, 8)), [], [V("wnt", 0, 16, 0, 8)])
-    pick(V("zq"), V("hr"), V("zoff"))
-    act(V("zqs"), V("hrs"), ACT.Copy, V("zoff"))
-    dma("y", "doc", T.oc[:, :], by(V("zq")), [], [V("zq")])
-    for k in range(4):
-        dma("s", "dos%d" % k, T.osc[4 * k:4 * k + 4, :], ap(V("zqs", 0, 128, 32 * k, 32 * k + 4)), [], [V("zqs")])
+    dma("s", "dwn", T.wn[:, :], ap(V("wnt", 0, 16, 0, 8)), [], [V("wnt", 0, 16, 0, 8)])
     finish()

@@ -4,37 +4,37 @@ from concourse.mybir import dt, AluOpType, AxisListType, ActivationFunctionType
 OP, ACT = AluOpType, ActivationFunctionType
 CAPP, CAPR = 48, 32
 LEAST = 128
-Z0 = 32
+Z0 = LEAST - CAPP
 END = Z0 + 8 * CAPP
-FULL = END + Z0
 FW = 144
+CUT = 64
 TW = 160
 BIG = 9e29
 BANK = 512
 
-SCRATCH = {"ps": ("psum", [128, 8 * BANK], "float32"), "we": ("sbuf", [32, 8], "int32"), "f0": ("sbuf", [32, 128], "bfloat16"),
+SCRATCH = {"ps": ("psum", [128, 8 * BANK], "float32"), "f0": ("sbuf", [32, 128], "bfloat16"),
            "zb": ("sbuf", [32, 128], "bfloat16"), "n4": ("sbuf", [128, 32], "bfloat16"),
-           "lt": ("sbuf", [32, 32], "float32"), "fr": ("sbuf", [32, 192], "float32"), "wn4": ("sbuf", [32, 32], "float32"),
-           "wnt": ("sbuf", [32, 32], "float32"), "wa": ("sbuf", [32, 8], "float32"), "wh": ("sbuf", [32, 8], "float32"),
-           "wz": ("sbuf", [32, 8], "float32"), "off": ("sbuf", [128, 24], "uint16"), "loff": ("sbuf", [128, 32], "uint16"),
-           "zoff": ("sbuf", [128, 8], "uint16"), "aboff": ("sbuf", [128, 8], "uint16"), "soff": ("sbuf", [128, 2], "uint16")}
-for _n, _w in (("xt", 512 + 4 * Z0), ("rtt", 512), ("wt", 2048), ("ut", 512), ("ur", 512), ("vt", 512), ("ones", 128),
-               ("ht", 4 * FULL), ("cb", 128), ("tmp", 128), ("tms", 384)):
+           "lt": ("sbuf", [32, 32], "float32"), "fr": ("sbuf", [32, 192], "bfloat16"),
+           "off": ("sbuf", [128, 24], "uint16"), "ooff": ("sbuf", [128, 4], "uint16"), "loff": ("sbuf", [128, 32], "uint16"),
+           "zoff": ("sbuf", [128, 8], "uint16"), "toff": ("sbuf", [128, 8], "uint16"), "aboff": ("sbuf", [128, 8], "uint16"),
+           "soff": ("sbuf", [128, 2], "uint16")}
+for _n, _w in (("xt", 512), ("zt", 512), ("rtt", 512), ("wt", 2048), ("ut", 512), ("ur", 512), ("vt", 512), ("ones", 128),
+               ("ht", 4 * END), ("cb", 128), ("tmp", 256), ("tms", 256), ("zw", TW), ("r8", 8), ("tr", 32), ("rk", TW),
+               ("nm", TW), ("ct", TW), ("ov", TW), ("role", TW), ("ma", TW), ("mb", TW), ("dd", FW), ("win", FW), ("cw", FW),
+               ("hf", FW)):
     SCRATCH[_n] = ("sbuf", [128, _w], "bfloat16")
-for _n, _w in (("xq", 128 + Z0), ("rq", 128), ("rp", 128), ("wq", 512), ("uq", 128), ("vq", 128), ("xd", 384), ("xr", FULL),
-               ("hq0", 192), ("hq1", 128), ("hq2", 128), ("hr", FULL), ("zq", 128)):
+for _n, _w in (("xq", 2 * LEAST), ("rq", 128), ("rp", 128), ("wq", 512), ("uq", 128), ("vq", 128), ("xd", 384), ("xn", 64),
+               ("xr", END), ("hq0", 192), ("hq1", 128), ("hq2", 128), ("hr", END), ("zq", 128)):
     SCRATCH[_n] = ("sbuf", [128, _w], "float8_e4m3fn_x4")
     SCRATCH[_n + "s"] = ("sbuf", [128, _w], "uint8")
 for _n, _w in (("ci", 224), ("cc", 224), ("c2", 4), ("bc", 1), ("sc", 1), ("bx", TW), ("pm", TW), ("zero", TW), ("d0", 64),
-               ("thr", 8), ("c8", 8), ("seg", 128), ("bs", 64), ("cp", 64), ("sg", 64), ("r8", 8), ("lc", 4), ("of", 32),
-               ("tr", 32), ("rk", TW), ("nm", TW), ("ct", TW), ("ov", TW), ("role", TW),
-               ("p1", TW), ("p2", TW), ("ma", TW), ("mb", TW), ("va", TW), ("vb", TW), ("ta", TW), ("tb", TW), ("lab", 256),
-               ("qw", END), ("yw", END), ("ga", FW), ("gb", FW), ("dd", FW), ("win", FW), ("cw", FW), ("hf", FW), ("xp", FW),
-               ("val", TW), ("tv", TW), ("s8", 128), ("ysb", 128)):
+               ("thr", 8), ("c8", 8), ("seg", 128), ("bs", 64), ("cp", 64), ("sg", 64), ("lc", 4), ("of", 32),
+               ("p1", TW), ("p2", TW), ("va", TW), ("vb", TW), ("ta", TW), ("tb", TW), ("lab", 256), ("tab", 2 * END),
+               ("qw", END), ("yw", END), ("ga", FW), ("gb", FW), ("xp", FW), ("val", TW), ("tv", TW), ("s8", 128),
+               ("wnr", 128), ("ysb", 128)):
     SCRATCH[_n] = ("sbuf", [128, _w], "float32")
-DMAS = ["dx", "drt", "dw0", "dw1", "du", "dv", "dxo", "dxos", "dzx", "dzxs", "dz", "dzs", "dze", "dzes", "dho", "dhos",
-        "doc", "dos0", "dos1", "dos2", "dos3", "dy", "dwn"]
-SEMAPHORES = ["cv", "cs", "ct", "cg", "ls", "xa0", "xa1", "xa2", "ha0", "ha1", "ha2"] + DMAS
+DMAS = ["dx", "drt", "dw0", "dw1", "du", "dv", "doc", "dos0", "dos1", "dos2", "dos3", "dy", "dwn"]
+SEMAPHORES = ["cv", "cs", "ct", "cg", "ls", "xn", "xa0", "xa1", "xa2", "ha0", "ha1", "ha2"] + DMAS
 
 
 def _runner(g, T):
@@ -112,15 +112,14 @@ def rank_program(g, core, T, topo):
     op, arrive, send, finish = _runner(g, T)
     N = len(T.cores)
 
-    chip = [topo.chip(c) for c in T.cores]
-    first, half = rank // 4, rank % 4 // 2
-    other = 4 * (1 - first)
+    def who(i):
+        return rank ^ i
+
     batch = []
-    for r0, n in ((4 * first, 4), (other + 2 * half, 2), (other + 2 * (1 - half), 2)):
-        c0, c1 = Z0 + CAPP * r0, Z0 + CAPP * (r0 + n)
-        more = max(LEAST - (c1 - c0), 0)
-        w0, w1 = (c0 - more, c1) if r0 % 4 == 0 else (c0, c1 + more)
-        batch.append((list(range(r0, r0 + n)), c0, c1, w0, w1))
+    for p0, n in ((0, 4), (4, 2), (6, 2)):
+        c0, c1 = Z0 + CAPP * p0, Z0 + CAPP * (p0 + n)
+        batch.append((list(range(p0, p0 + n)), c0, c1, min(c0, c1 - LEAST), c1))
+    chip = [topo.chip(c) for c in T.cores]
     away = topo.engines(core, next(c for c in T.cores if topo.chip(c) != topo.chip(core)))
     peer = next(c for c in T.cores if topo.chip(c) == topo.chip(core) and c != core)
     near = [e for e in topo.engines(core, peer) if e not in away][:len(away) // 2]
@@ -187,9 +186,9 @@ def rank_program(g, core, T, topo):
     def turn(out, in_):
         op("v", lambda q: q.transpose(ap(out), ap(in_)), [out], [in_])
 
-    def quant(c, t, a=0, b=None):
+    def quant(c, t, a=0, b=None, d=0):
         n = SCRATCH[t][1][1] // 4 if b is None else b - a
-        o, s, i = V(c, 0, n), V(c + "s", 0, n), V(t, 4 * a, 4 * (a + n))
+        o, s, i = V(c, d, d + n), V(c + "s", d, d + n), V(t, 4 * a, 4 * (a + n))
         op("v", lambda q: q.quantize_mx(ap(o), ap(s), ap(i)), [o, s], [i])
 
     def mm(bank, l, la, r, ra, rb):
@@ -202,13 +201,8 @@ def rank_program(g, core, T, topo):
     def dma(q, sem, dst, src, outs, ins):
         op(q, lambda e: e.dma_start(dst, src), outs, ins, dma=sem)
 
-    def move(sems, dst, da, src, sa, n):
-        for sem, x, f in ((sems, "", by), (sems + "s", "s", ap)):
-            o, i = V(dst + x, da, da + n), V(src + x, sa, sa + n)
-            dma("y", sem, f(o), f(i), [o], [i])
-
     dma("s", "drt", ap(V("rtt", 0, 4 * N)), T.rt[:, 0:4 * N], [V("rtt", 0, 4 * N)], [])
-    dma("y", "dx", ap(V("xt", 0, 512)), T.x[:, :], [V("xt", 0, 512)], [])
+    dma("y", "dx", ap(V("xt")), T.x[:, :], [V("xt")], [])
     dma("y", "dv", ap(V("vt")), T.v[:, :], [V("vt")], [])
     dma("y", "dw0", ap(V("wt", 0, 1024)), T.w[:, 0:1024], [V("wt", 0, 1024)], [])
     dma("y", "dw1", ap(V("wt", 1024, 2048)), T.w[:, 1024:2048], [V("wt", 1024, 2048)], [])
@@ -216,6 +210,9 @@ def rank_program(g, core, T, topo):
 
     def iota(v, pattern, b, cm=0):
         op("g", lambda q: q.iota(ap(v), pattern, b, cm, allow_small_or_imprecise_dtypes=True), [v], [])
+
+    def steps(w):
+        return [[-w * b if rank & b else w * b, 2] for b in (4, 2, 1)], w * rank
 
     iota(V("ci", 0, 32), [[0, 4], [1, 8]], 0)
     iota(V("ci", 32, 64), [[0, 2], [1, 2], [0, 8]], 0)
@@ -225,34 +222,34 @@ def rank_program(g, core, T, topo):
     iota(V("ci", 96, 128), [[0, 8], [1, 4]], 0)
     iota(V("thr"), [[-1, 8]], 7)
     iota(V("c8"), [[-1, 8]], 8)
-    iota(V("ci", 128, 160), [[0, 4], [CAPP, 8]], Z0 - 1)
+    up, at = steps(CAPP)
+    for k in range(4):
+        iota(V("ci", 128 + 8 * k, 136 + 8 * k), up, Z0 - 1 + at)
     iota(V("ci", 160, 192), [[0, 2], [1, 2], [0, 8]], -1)
     iota(V("ci", 192, 224), [[16, 2], [16, 16]], -1)
     iota(V("bx"), [[0, 5], [1, 2], [0, 16]], 0)
     ecol, hcol, mcol, pcol, gcol, lcol = (V("cc", c, c + 1) for c in (0, 32, 96, 128, 160, 192))
-    memset(V("rtt", 4 * N, 512), 0.0)
     memset(V("zero"), 0.0)
+    memset(V("rtt", 4 * N, 512), 0.0)
     memset(V("d0"), 1.0)
-    turn(V("cc", 0, 64), V("ci", 0, 64))
-    memset(V("zb"), 0.0)
     memset(V("d0", 9, 64, st=9), -1.0)
-    memset(V("xt", 512, 512 + 4 * Z0), 0.0)
+    memset(V("d0", 0, 64, st=8), 0.0)
+    turn(V("cc", 0, 64), V("ci", 0, 64))
     ts(V("aboff", 0, 4), V("c2"), hcol, OP.add, ecol, OP.min)
     ts(V("aboff", 4, 8), V("c2"), hcol, OP.add, ecol, OP.max)
-    memset(V("d0", 0, 64, st=8), 0.0)
-    turn(V("cc", 64, 128), V("ci", 64, 128))
+    for c in range(0, 512, TW):
+        fill(V("zt", c, min(c + TW, 512)), 0.0)
     fill(V("n4", 24, 32), 0.0)
-    for c0 in (0, 160):
-        fill(V("fr", c0, c0 + 32), 8.0)
-    fill(V("qw", 0, Z0), -BIG)
-    fill(V("yw", 0, Z0), 0.0)
+    fill(V("zb"), 0.0)
 
     quant("rq", "rtt")
     pick(V("rp"), V("rq"), V("aboff"))
     act(V("rps"), V("rqs"), ACT.Copy, V("aboff"))
-    quant("xq", "xt")
+    quant("xq", "xt", 0, LEAST)
     mm(0, "xq", 0, "rp", 0, 128)
-    ts(V("bc"), mcol, 0.5, OP.is_ge, 64.0, OP.mult)
+    quant("xq", "zt", 0, LEAST, LEAST)
+    turn(V("cc", 64, 128), V("ci", 64, 128))
+    ts(V("bc"), mcol, 1.5, OP.is_ge, 64.0, OP.mult)
     copy(V("bs"), V("ps", 64, 128))
     tt(V("cp"), V("ps", 0, 64), V("bs"), OP.is_ge)
     runs(V("sg"), V("d0"), V("cp"))
@@ -260,6 +257,16 @@ def rank_program(g, core, T, topo):
     for k in range(3):
         tt(V("n4", k, 24, st=3), rank8, V("thr"), OP.is_ge)
     tt(V("r8"), V("c8"), rank8, OP.subtract)
+    for c0 in (0, 160):
+        fill(V("fr", c0, c0 + 32), 8.0)
+    fill(V("zw"), 0.0)
+    for c in range(0, 4 * Z0, TW):
+        fill(V("ht", c, c + TW), 0.0)
+    fill(V("val", FW, TW), 0.0)
+    fill(V("seg"), 1.0)
+    fill(V("qw", 0, Z0), -BIG)
+    fill(V("yw", 0, Z0), 0.0)
+    fill(V("seg", 0, 128, st=16), 0.0)
     for a in range(4):
         turn(V("f0", 32 * a, 32 * a + 32), V("n4", 0, 32, 32 * a, 32 * a + 32))
     ts(V("sc"), V("bc"), -1.0 / 128, OP.mult, 1.0, OP.add)
@@ -267,10 +274,12 @@ def rank_program(g, core, T, topo):
         scan(V("cb", 0, 128, 32 * a, 32 * a + 32), V("f0"), V("zb"), V("cc", 64 + a, 65 + a, 0, 32))
     for j in range(4):
         copy(V("tr", 8 * j, 8 * j + 8), V("r8"), "s")
-    for m in (1, 2, 3):
-        act(V("tms", 128 * (m - 1), 128 * m), V("cb"), ACT.Sign, acc=V("lc", m, m + 1), bias=m + 0.5, scale=-1.0)
-    ts(V("tmp"), V("cb"), 0.0, OP.is_le)
-    total(V("lc", 0, 1), V("tmp"))
+    for m in (2, 3):
+        act(V("tms", 128 * m - 256, 128 * m - 128), V("cb"), ACT.Sign, acc=V("lc", m, m + 1), bias=m + 0.5, scale=-1.0)
+    for m in (0, 1):
+        ts(V("tmp", 128 * m, 128 * m + 128), V("cb"), float(m), OP.is_le)
+    for m in (0, 1):
+        total(V("lc", m, m + 1), V("tmp", 128 * m, 128 * m + 128))
     for a in range(4):
         for d in (0, 16):
             copy(V("lt", d + 4 * a, d + 4 * a + 4), V("lc", 0, 4, 32 * a, 32 * a + 32), "s" if d else "v")
@@ -278,20 +287,19 @@ def rank_program(g, core, T, topo):
         turn(V("of", 0, 32, 32 * a, 32 * a + 32), V("lt"))
     ts(V("off"), V("of", 0, 24), V("sc"), OP.mult, V("bc"), OP.add)
 
-    def parts(h):
-        to = [r for r in batch[h][0] if r != rank]
-        far = [r for r in to if chip[r] != topo.chip(core)]
-        return to, far, len(away) // len(far)
+    def parts(places):
+        to = [i for i in places if i > 0]
+        far = [i for i in to if chip[who(i)] != topo.chip(core)]
+        return to, far, len(away) // max(len(far), 1)
 
-    def ship(h, src, s0, dst, sem):
-        to, far, k = parts(h)
-        d0 = Z0 + CAPP * rank
+    def ship(places, src, s0, dst, sem):
+        to, far, k = parts(places)
         for x, f in (("", by), ("s", ap)):
             trs, ins, ls = [], [], 0
-            for r in to:
-                eng = near if r not in far else away[k * far.index(r):k * far.index(r) + k]
-                rid, pid, _s = topo.addr(T.cores[r])
-                a = Z0 + CAPP * r - s0
+            for i in to:
+                eng = near if i not in far else away[k * far.index(i):k * far.index(i) + k]
+                rid, pid, _s = topo.addr(T.cores[who(i)])
+                a, d0 = s0(i), Z0 + CAPP * i
                 s, d = V(src + x, a, a + CAPP), V(dst + x, d0, d0 + CAPP)
                 trs.append(RemoteDMATransfer(dst_ids=[DstId(rid=rid, pnc=pid)], dma_engine_mask=bits(eng), remote_sem=T.sem[sem],
                                              src=f(s), dst=f(d)))
@@ -299,54 +307,63 @@ def rank_program(g, core, T, topo):
                 ls += len(eng)
             send(lambda q: q.remote_dma_fused(trs, local_sem=T.sem["ls"]), ins, ls)
 
-    def land(h, dst, sem):
-        to, far, k = parts(h)
+    def land(places, dst, sem):
+        to, far, k = parts(places)
         n = 2 * (len(far) * k + len(near) * (len(to) - len(far)))
-        arrive(sem, n, [V(dst + x, Z0 + CAPP * r, Z0 + CAPP * r + CAPP) for r in to for x in ("", "s")])
+        arrive(sem, n, [V(dst + x, Z0 + CAPP * i, Z0 + CAPP * i + CAPP) for i in to for x in ("", "s")])
 
-    for h, (_rs, c0, c1, _w0, _w1) in enumerate(batch):
-        a, b = c0 - Z0, c1 - Z0
-        lst = V("off", a // 16, b // 16)
-        pick(V("xd", a, b), V("xq"), lst)
-        act(V("xds", a, b), V("xqs"), ACT.Copy, lst)
-        ship(h, "xd", Z0, "xr", "xa%d" % h)
-        if h == 0:
-            move("dxo", "xr", Z0 + CAPP * rank, "xd", CAPP * rank, CAPP)
-            move("dzx", "xr", END if first == 0 else 0, "xq", 128, Z0)
-            move("dz", "hr", 0, "xq", 128, Z0)
-            if first == 0:
-                move("dze", "hr", END, "xq", 128, Z0)
+    def picks(dst, d, lst):
+        n = 16 * (lst[4] - lst[3])
+        pick(V(dst, d, d + n), V("xq"), lst)
+        act(V(dst + "s", d, d + n), V("xqs"), ACT.Copy, lst)
+
+    def pair(i):
+        e = who(i) // 2 * 2
+        picks("xd", CAPP * e, V("off", 3 * e, 3 * e + 6))
+
+    pair(2)
+    ship([2, 3], "xd", lambda i: CAPP * who(i), "xr", "xa0")
+    pr = who(1)
+    picks("xn", 0, V("off", 3 * pr - pr % 2, 3 * pr + 3))
+    ship([1], "xn", lambda i: 16 * (pr % 2), "xr", "xn")
+    for h in (1, 2):
+        pair(batch[h][0][0])
+        ship(batch[h][0], "xd", lambda i: CAPP * who(i), "xr", "xa%d" % h)
+    if rank % 2:
+        copy(V("ooff", 0, 3), V("off", 3 * rank, 3 * rank + 3))
+    picks("xr", Z0, V("ooff", 0, 3) if rank % 2 else V("off", 3 * rank, 3 * rank + 3))
+
+    up, at = steps(1)
+    iota(V("tab", END - Z0, END + Z0 - 1), [[0, 2 * Z0 - 1]], -100)
+    for b in (0, 1):
+        c = END - 1 + Z0 + 4 * CAPP * b
+        iota(V("tab", c, c + 4 * CAPP), up[1:] + [[0, CAPP]], at + b * up[0][0])
+        c = 4 * CAPP * b
+        iota(V("tab", c, c + 4 * CAPP), up[1:] + [[0, CAPP]], -1 - who(7) + b * up[0][0])
 
     for a in range(4):
         turn(V("fr", 32 + 32 * a, 64 + 32 * a), V("tr", 0, 32, 32 * a, 32 * a + 32))
-    memset(V("ones"), 1.0)
     quant("wq", "wt")
-    for t in range(4):
-        ts(V("ur", t, 512, st=4), V("ones"), V("ut", t, t + 1), OP.mult)
     turn(V("cc", 128, 224), V("ci", 128, 224))
     for a in range(4):
-        q = "v" if a == 3 else "s"
-        copy(V("rk", 0, TW, 32 * a, 32 * a + 32), V("fr", 32, 192), q)
-        if a == 3:
-            quant("uq", "ur")
-        copy(V("rk", 0, TW, 32 * a, 32 * a + 16), V("fr", 16, 176, 0, 16), q)
+        copy(V("rk", 0, TW, 32 * a, 32 * a + 32), V("fr", 32, 192), "v" if a > 1 else "s")
+    for a in range(4):
+        copy(V("rk", 0, TW, 32 * a, 32 * a + 16), V("fr", 16, 176, 0, 16), "v" if a > 1 else "s")
     act(V("pm"), V("bx"), ACT.Abs, bias=gcol)
+    memset(V("ones"), 1.0)
+    ts(V("nm"), V("rk"), 1.0, OP.is_le)
+    for t in range(4):
+        ts(V("ur", t, 512, st=4), V("ones"), V("ut", t, t + 1), OP.mult)
+    scan(V("ct"), V("nm"), V("zw"), 0.0)
+    quant("uq", "ur")
+    act(V("p1"), V("ct"), ACT.Identity, bias=pcol)
+    act(V("ov"), V("ct"), ACT.Relu, scale=2.0, bias=-2.0 * CAPP)
     ts(V("soff", 0, 1), lcol, 0.0, OP.max, 255.0, OP.min)
     ts(V("soff", 1, 2), lcol, 128.0, OP.add, 255.0, OP.min)
-    ts(V("nm"), V("rk"), 1.0, OP.is_le)
-    scan(V("ct"), V("nm"), V("zero"), 0.0)
-    quant("vq", "vt")
-    act(V("ov"), V("ct"), ACT.Relu, scale=2.0, bias=-2.0 * CAPP)
-    ts(V("p1"), V("ct"), pcol, OP.add)
-    m0 = END if first == 0 else 0
-    fill(V("ht", 4 * m0, 4 * m0 + 4 * Z0), 0.0)
-    fill(V("val", FW, TW), 0.0)
-    fill(V("wn4"), 0.0)
-    fill(V("seg"), 1.0)
-    fill(V("seg", 0, 128, st=16), 0.0)
 
-    for h, (_rs, c0, c1, w0, w1) in enumerate(batch):
-        land(h, "xr", "xa%d" % h)
+    land([1], "xr", "xn")
+    for h, (places, c0, c1, w0, w1) in enumerate(batch):
+        land([i for i in places if i > 1], "xr", "xa%d" % h)
         banks = [4 * (h % 2) + i for i in range(4)]
         for i in (0, 2, 1, 3):
             mm(banks[i], "wq", 128 * i, "xr", w0, w1)
@@ -356,57 +373,61 @@ def rank_program(g, core, T, topo):
                 ts(o, r, 0.0, OP.max, 0.0625, OP.mult)
             else:
                 act(o, r, ACT.Relu, scale=0.0625)
-        hq = "hq%d" % h
-        quant(hq, "ht", w0, w1)
-        ship(h, hq, w0, "hr", "ha%d" % h)
+        quant("hq%d" % h, "ht", w0, w1)
+        ship(places, "hq%d" % h, lambda i: Z0 + CAPP * i - w0, "hr", "ha%d" % h)
         if h == 0:
-            move("dho", "hr", Z0 + CAPP * rank, hq, Z0 + CAPP * rank - w0, CAPP)
+            quant("hr", "ht", 0, LEAST)
+            tt(V("role"), V("rk"), V("ov"), OP.add)
+        elif h == 1:
+            tt(V("p2"), V("p1"), V("pm"), OP.mult)
 
-    tt(V("role"), V("rk"), V("ov"), OP.add)
-    tt(V("p2"), V("p1"), V("pm"), OP.mult)
-    act(V("ma"), V("role"), ACT.Relu, scale=-1.0, bias=1.0)
     ts(V("mb"), V("role"), 1.0, OP.is_equal)
+    ts(V("ma"), V("role"), 0.0, OP.is_equal)
     tt(V("vb"), V("mb"), V("p2"), OP.mult)
     tt(V("va"), V("ma"), V("p2"), OP.mult)
     turn(V("tb"), V("vb"))
     turn(V("ta"), V("va"))
     runs(V("lab", 128, 256), V("seg"), V("tb", 8, 136))
     runs(V("lab", 0, 128), V("seg"), V("ta", 8, 136))
+    quant("vq", "vt")
     copy(V("loff"), V("lab"), "v", V("soff"))
 
     last = len(batch) - 1
-    for h, (_rs, c0, c1, w0, w1) in enumerate(batch):
-        land(h, "hr", "ha%d" % h)
+    cuts = ((0, CUT), (CUT, FW))
+    for h, (places, c0, c1, w0, w1) in enumerate(batch):
+        land(places, "hr", "ha%d" % h)
         mm(h, "uq", 0, "hr", w0, w1)
-        mm(3 + h, "vq", 0, "hr", w0, w1)
+        mm(4 + h, "vq", 0, "hr", w0, w1)
         copy(V("qw", c0, c1), V("ps", BANK * h + c0 - w0, BANK * h + c1 - w0), "v" if h == last else "s")
         if h == last:
-            copy(V("ga"), V("qw"), "v", V("loff", 0, 9))
-            copy(V("gb"), V("qw"), "s", V("loff", 16, 25))
-        copy(V("yw", c0, c1), V("ps", BANK * (3 + h) + c0 - w0, BANK * (3 + h) + c1 - w0), "s")
-    tt(V("dd"), V("gb"), V("ga"), OP.is_gt)
-    tt(V("win"), V("dd"), V("role", 0, FW), OP.is_equal)
-    scan(V("cw"), V("win"), V("zero", 0, FW), 0.0)
-    act(V("hf"), V("cw"), ACT.Sign, bias=CAPR + 0.5, scale=-1.0)
-    tt(V("xp"), V("win"), V("p2", 0, FW), OP.mult)
-    tt(V("val", 0, FW), V("xp"), V("hf"), OP.mult)
-    turn(V("tv"), V("val"))
-    runs(V("s8"), V("seg"), V("tv", 8, 136))
-    copy(V("zoff"), V("s8", 15, 128, st=16))
+            for a, b in cuts:
+                copy(V("ga", a, b), V("qw"), "v", V("loff", a // 16, b // 16))
+                copy(V("gb", a, b), V("qw"), "s", V("loff", 16 + a // 16, 16 + b // 16))
+        copy(V("yw", c0, c1), V("ps", BANK * (4 + h) + c0 - w0, BANK * (4 + h) + c1 - w0), "s")
+    for a, b in cuts:
+        tt(V("dd", a, b), V("gb", a, b), V("ga", a, b), OP.is_gt)
+    for a, b in cuts:
+        tt(V("win", a, b), V("dd", a, b), V("role", a, b), OP.is_equal)
+    for a, b in cuts:
+        scan(V("cw", a, b), V("win", a, b), V("zw", a, b), V("cw", a - 1, a) if a else 0.0)
+        act(V("hf", a, b), V("cw", a, b), ACT.Sign, bias=CAPR + 0.5, scale=-1.0)
+        tt(V("xp", a, b), V("win", a, b), V("p2", a, b), OP.mult)
+    for a, b in cuts:
+        tt(V("val", a, b), V("xp", a, b), V("hf", a, b), OP.mult)
+    turn(V("tv", 0, CUT), V("val", 0, CUT))
+    turn(V("tv", CUT, TW), V("val", CUT, TW))
+    for a, b in ((0, CUT - 16), (CUT - 16, 128)):
+        runs(V("s8", a, b), V("seg", a, b), V("tv", 8 + a, 8 + b))
+    s = V("s8", 15, 128, st=16)
+    copy(V("zoff"), s)
+    ts(V("toff"), s, float(END - 1), OP.add)
+    pick(V("zq"), V("hr"), V("zoff"))
+    dma("y", "doc", T.oc[:, :], by(V("zq")), [], [V("zq")])
     act(V("ysb"), V("yw"), ACT.Copy, V("zoff"))
     dma("y", "dy", T.y[:, :], ap(V("ysb")), [], [V("ysb")])
-    s = V("s8", 15, 128, 0, 32, 16)
-    mid = (Z0 + (CAPP - 1) / 2.0) / CAPP
-    ts(V("wa"), s, 1.0 / CAPP, OP.mult, mid - 1.0, OP.add)
-    ts(V("wh"), s, 1.0, OP.is_ge, 1.0 - 2.0 * mid, OP.mult)
-    ts(V("wz"), s, 0.0, OP.is_equal, -100.0, OP.mult)
-    pick(V("zq"), V("hr", 0, END), V("zoff"))
-    dma("y", "doc", T.oc[:, :], by(V("zq")), [], [V("zq")])
-    act(V("zqs"), V("hrs", 0, END), ACT.Copy, V("zoff"))
+    copy(V("zqs"), V("hrs"), "v", V("zoff"))
+    act(V("wnr"), V("tab", 0, 2 * END - 1), ACT.Copy, V("toff"))
     for k in range(4):
         dma("s" if k < 2 else "y", "dos%d" % k, T.osc[4 * k:4 * k + 4, :], ap(V("zqs", 0, 128, 32 * k, 32 * k + 4)), [], [V("zqs")])
-    tt(V("we"), V("wa"), V("wh"), OP.add)
-    tt(V("wn4", 0, 8), V("we"), V("wz"), OP.add)
-    turn(V("wnt"), V("wn4"))
-    dma("s", "dwn", T.wn[:, :], ap(V("wnt", 0, 16, 0, 8)), [], [V("wnt", 0, 16, 0, 8)])
+    dma("s", "dwn", T.wn[:, :], ap(V("wnr", 0, 128, 0, 1)), [], [V("wnr", 0, 128, 0, 1)])
     finish()

@@ -7,7 +7,7 @@ LEAST = 128
 Z0 = LEAST - CAPP
 END = Z0 + 8 * CAPP
 FW = 144
-CUT = 64
+CUT = 96
 TW = 160
 BIG = 9e29
 BANK = 512
@@ -15,26 +15,26 @@ BANK = 512
 SCRATCH = {"ps": ("psum", [128, 8 * BANK], "float32"), "f0": ("sbuf", [32, 128], "bfloat16"),
            "zb": ("sbuf", [32, 128], "bfloat16"), "n4": ("sbuf", [128, 32], "bfloat16"),
            "lt": ("sbuf", [32, 32], "float32"), "fr": ("sbuf", [32, 192], "bfloat16"),
-           "off": ("sbuf", [128, 24], "uint16"), "ooff": ("sbuf", [128, 4], "uint16"), "loff": ("sbuf", [128, 32], "uint16"),
-           "zoff": ("sbuf", [128, 8], "uint16"), "toff": ("sbuf", [128, 8], "uint16"), "aboff": ("sbuf", [128, 8], "uint16"),
-           "soff": ("sbuf", [128, 2], "uint16")}
-for _n, _w in (("xt", 512), ("zt", 512), ("rtt", 512), ("wt", 2048), ("ut", 512), ("ur", 512), ("vt", 512), ("ones", 128),
+           "off": ("sbuf", [128, 24], "uint16"), "ooff": ("sbuf", [128, 4], "uint16"), "poff": ("sbuf", [128, 4], "uint16"),
+           "loff": ("sbuf", [128, 32], "uint16"), "zoff": ("sbuf", [128, 8], "uint16"), "toff": ("sbuf", [128, 8], "uint16"),
+           "aboff": ("sbuf", [128, 8], "uint16"), "soff": ("sbuf", [128, 2], "uint16")}
+for _n, _w in (("xt", 512), ("zt", 512), ("rtt", 512), ("wt", 2048), ("ut", 512), ("ur", 512), ("vt", 512),
                ("ht", 4 * END), ("cb", 128), ("tmp", 256), ("tms", 256), ("zw", TW), ("r8", 8), ("tr", 32), ("rk", TW),
-               ("nm", TW), ("ct", TW), ("ov", TW), ("role", TW), ("ma", TW), ("mb", TW), ("dd", FW), ("win", FW), ("cw", FW),
+               ("nm", FW), ("ct", FW), ("ov", FW), ("role", FW), ("ma", FW), ("mb", FW), ("dd", FW), ("win", FW), ("cw", FW),
                ("hf", FW)):
     SCRATCH[_n] = ("sbuf", [128, _w], "bfloat16")
-for _n, _w in (("xq", 2 * LEAST), ("rq", 128), ("rp", 128), ("wq", 512), ("uq", 128), ("vq", 128), ("xd", 384), ("xn", 64),
-               ("xr", END), ("hq0", 192), ("hq1", 128), ("hq2", 128), ("hr", END), ("zq", 128)):
+for _n, _w in (("xq", 2 * LEAST), ("rq", 128), ("rp", 128), ("wq", 512), ("uq", 128), ("vq", 128), ("xd", 384),
+               ("xf", LEAST + 2), ("xr", END), ("hq0", 192), ("hq1", 128), ("hq2", 128), ("hr", END), ("zq", 128)):
     SCRATCH[_n] = ("sbuf", [128, _w], "float8_e4m3fn_x4")
     SCRATCH[_n + "s"] = ("sbuf", [128, _w], "uint8")
-for _n, _w in (("ci", 224), ("cc", 224), ("c2", 4), ("bc", 1), ("sc", 1), ("bx", TW), ("pm", TW), ("zero", TW), ("d0", 64),
+for _n, _w in (("ci", 224), ("cc", 224), ("c2", 4), ("bc", 1), ("sc", 1), ("bx", FW), ("pm", FW), ("zero", TW), ("d0", 64),
                ("thr", 8), ("c8", 8), ("seg", 128), ("bs", 64), ("cp", 64), ("sg", 64), ("lc", 4), ("of", 32),
-               ("p1", TW), ("p2", TW), ("va", TW), ("vb", TW), ("ta", TW), ("tb", TW), ("lab", 256), ("tab", 2 * END),
+               ("p1", FW), ("p2", FW), ("va", TW), ("vb", TW), ("ta", TW), ("tb", TW), ("lab", 256), ("tab", 2 * END),
                ("qw", END), ("yw", END), ("ga", FW), ("gb", FW), ("xp", FW), ("val", TW), ("tv", TW), ("s8", 128),
                ("wnr", 128), ("ysb", 128)):
     SCRATCH[_n] = ("sbuf", [128, _w], "float32")
 DMAS = ["dx", "drt", "dw0", "dw1", "du", "dv", "doc", "dos0", "dos1", "dos2", "dos3", "dy", "dwn"]
-SEMAPHORES = ["cv", "cs", "ct", "cg", "ls", "xn", "xa0", "xa1", "xa2", "ha0", "ha1", "ha2"] + DMAS
+SEMAPHORES = ["cv", "cs", "ct", "cg", "ls", "xf", "xl", "xa0", "xa1", "xa2", "ha0", "ha1", "ha2"] + DMAS
 
 
 def _runner(g, T):
@@ -122,7 +122,8 @@ def rank_program(g, core, T, topo):
     chip = [topo.chip(c) for c in T.cores]
     away = topo.engines(core, next(c for c in T.cores if topo.chip(c) != topo.chip(core)))
     peer = next(c for c in T.cores if topo.chip(c) == topo.chip(core) and c != core)
-    near = [e for e in topo.engines(core, peer) if e not in away][:len(away) // 2]
+    every = topo.engines(core, peer)
+    near = [e for e in every if e not in away][:len(away) // 2]
 
     def bits(es):
         return sum(1 << e for e in es)
@@ -198,8 +199,43 @@ def rank_program(g, core, T, topo):
     def pick(o, w, lst):
         op("v", lambda q: q.tensor_copy(ap(o).bitcast(dt.uint32), ap(w).bitcast(dt.uint32).indirect(ap(lst))), [o], [w, lst])
 
+    def picks(dst, d, lst, src="xq"):
+        n = 16 * (lst[4] - lst[3])
+        pick(V(dst, d, d + n), V(src), lst)
+        act(V(dst + "s", d, d + n), V(src + "s"), ACT.Copy, lst)
+
     def dma(q, sem, dst, src, outs, ins):
         op(q, lambda e: e.dma_start(dst, src), outs, ins, dma=sem)
+
+    def transfer(to, eng, sem, src, dst):
+        rid, pid, _s = topo.addr(to)
+        return RemoteDMATransfer(dst_ids=[DstId(rid=rid, pnc=pid)], dma_engine_mask=bits(eng), remote_sem=T.sem[sem], src=src, dst=dst)
+
+    def to_peer(eng, sem, s, d, f):
+        send(lambda q: q.remote_dma_fused([transfer(peer, eng, sem, f(s), f(d))], local_sem=T.sem["ls"]), [s], len(eng))
+
+    def parts(places):
+        to = [i for i in places if i > 0]
+        far = [i for i in to if chip[who(i)] != topo.chip(core)]
+        return to, far, len(away) // max(len(far), 1)
+
+    def ship(places, src, s0, dst, sem):
+        to, far, k = parts(places)
+        for x, f in (("", by), ("s", ap)):
+            trs, ins, ls = [], [], 0
+            for i in to:
+                eng = near if i not in far else away[k * far.index(i):k * far.index(i) + k]
+                a, d0 = s0(i), Z0 + CAPP * i
+                s, d = V(src + x, a, a + CAPP), V(dst + x, d0, d0 + CAPP)
+                trs.append(transfer(T.cores[who(i)], eng, sem, f(s), f(d)))
+                ins.append(s)
+                ls += len(eng)
+            send(lambda q: q.remote_dma_fused(trs, local_sem=T.sem["ls"]), ins, ls)
+
+    def land(places, dst, sem):
+        to, far, k = parts(places)
+        n = 2 * (len(far) * k + len(near) * (len(to) - len(far)))
+        arrive(sem, n, [V(dst + x, Z0 + CAPP * i, Z0 + CAPP * i + CAPP) for i in to for x in ("", "s")])
 
     dma("s", "drt", ap(V("rtt", 0, 4 * N)), T.rt[:, 0:4 * N], [V("rtt", 0, 4 * N)], [])
     dma("y", "dx", ap(V("xt")), T.x[:, :], [V("xt")], [])
@@ -222,12 +258,8 @@ def rank_program(g, core, T, topo):
     iota(V("ci", 96, 128), [[0, 8], [1, 4]], 0)
     iota(V("thr"), [[-1, 8]], 7)
     iota(V("c8"), [[-1, 8]], 8)
-    up, at = steps(CAPP)
-    for k in range(4):
-        iota(V("ci", 128 + 8 * k, 136 + 8 * k), up, Z0 - 1 + at)
     iota(V("ci", 160, 192), [[0, 2], [1, 2], [0, 8]], -1)
     iota(V("ci", 192, 224), [[16, 2], [16, 16]], -1)
-    iota(V("bx"), [[0, 5], [1, 2], [0, 16]], 0)
     ecol, hcol, mcol, pcol, gcol, lcol = (V("cc", c, c + 1) for c in (0, 32, 96, 128, 160, 192))
     memset(V("zero"), 0.0)
     memset(V("rtt", 4 * N, 512), 0.0)
@@ -248,11 +280,13 @@ def rank_program(g, core, T, topo):
     quant("xq", "xt", 0, LEAST)
     mm(0, "xq", 0, "rp", 0, 128)
     quant("xq", "zt", 0, LEAST, LEAST)
-    turn(V("cc", 64, 128), V("ci", 64, 128))
-    ts(V("bc"), mcol, 1.5, OP.is_ge, 64.0, OP.mult)
+    to_peer(every, "xf", V("xq", 0, LEAST + 2), V("xf"), by)
+    to_peer(every, "xf", V("xqs", 0, LEAST + 2), V("xfs"), ap)
     copy(V("bs"), V("ps", 64, 128))
+    turn(V("cc", 64, 128), V("ci", 64, 128))
     tt(V("cp"), V("ps", 0, 64), V("bs"), OP.is_ge)
     runs(V("sg"), V("d0"), V("cp"))
+    ts(V("bc"), mcol, 1.5, OP.is_ge, 64.0, OP.mult)
     rank8 = V("sg", 7, 64, st=8)
     for k in range(3):
         tt(V("n4", k, 24, st=3), rank8, V("thr"), OP.is_ge)
@@ -262,7 +296,8 @@ def rank_program(g, core, T, topo):
     fill(V("zw"), 0.0)
     for c in range(0, 4 * Z0, TW):
         fill(V("ht", c, c + TW), 0.0)
-    fill(V("val", FW, TW), 0.0)
+    for b in ("val", "va", "vb"):
+        fill(V(b, FW, TW), 0.0)
     fill(V("seg"), 1.0)
     fill(V("qw", 0, Z0), -BIG)
     fill(V("yw", 0, Z0), 0.0)
@@ -276,92 +311,55 @@ def rank_program(g, core, T, topo):
         copy(V("tr", 8 * j, 8 * j + 8), V("r8"), "s")
     for m in (2, 3):
         act(V("tms", 128 * m - 256, 128 * m - 128), V("cb"), ACT.Sign, acc=V("lc", m, m + 1), bias=m + 0.5, scale=-1.0)
+    turn(V("cc", 160, 224), V("ci", 160, 224))
     for m in (0, 1):
         ts(V("tmp", 128 * m, 128 * m + 128), V("cb"), float(m), OP.is_le)
     for m in (0, 1):
         total(V("lc", m, m + 1), V("tmp", 128 * m, 128 * m + 128))
+    ts(V("soff", 0, 1), lcol, 0.0, OP.max, 255.0, OP.min)
     for a in range(4):
         for d in (0, 16):
             copy(V("lt", d + 4 * a, d + 4 * a + 4), V("lc", 0, 4, 32 * a, 32 * a + 32), "s" if d else "v")
+    ts(V("soff", 1, 2), lcol, 128.0, OP.add, 255.0, OP.min)
     for a in range(4):
         turn(V("of", 0, 32, 32 * a, 32 * a + 32), V("lt"))
     ts(V("off"), V("of", 0, 24), V("sc"), OP.mult, V("bc"), OP.add)
 
-    def parts(places):
-        to = [i for i in places if i > 0]
-        far = [i for i in to if chip[who(i)] != topo.chip(core)]
-        return to, far, len(away) // max(len(far), 1)
-
-    def ship(places, src, s0, dst, sem):
-        to, far, k = parts(places)
-        for x, f in (("", by), ("s", ap)):
-            trs, ins, ls = [], [], 0
-            for i in to:
-                eng = near if i not in far else away[k * far.index(i):k * far.index(i) + k]
-                rid, pid, _s = topo.addr(T.cores[who(i)])
-                a, d0 = s0(i), Z0 + CAPP * i
-                s, d = V(src + x, a, a + CAPP), V(dst + x, d0, d0 + CAPP)
-                trs.append(RemoteDMATransfer(dst_ids=[DstId(rid=rid, pnc=pid)], dma_engine_mask=bits(eng), remote_sem=T.sem[sem],
-                                             src=f(s), dst=f(d)))
-                ins.append(s)
-                ls += len(eng)
-            send(lambda q: q.remote_dma_fused(trs, local_sem=T.sem["ls"]), ins, ls)
-
-    def land(places, dst, sem):
-        to, far, k = parts(places)
-        n = 2 * (len(far) * k + len(near) * (len(to) - len(far)))
-        arrive(sem, n, [V(dst + x, Z0 + CAPP * i, Z0 + CAPP * i + CAPP) for i in to for x in ("", "s")])
-
-    def picks(dst, d, lst):
-        n = 16 * (lst[4] - lst[3])
-        pick(V(dst, d, d + n), V("xq"), lst)
-        act(V(dst + "s", d, d + n), V("xqs"), ACT.Copy, lst)
-
-    def pair(i):
+    def pair(i, sem):
         e = who(i) // 2 * 2
         picks("xd", CAPP * e, V("off", 3 * e, 3 * e + 6))
+        ship([i, i + 1], "xd", lambda j: CAPP * who(j), "xr", sem)
 
-    pair(2)
-    ship([2, 3], "xd", lambda i: CAPP * who(i), "xr", "xa0")
-    pr = who(1)
-    picks("xn", 0, V("off", 3 * pr - pr % 2, 3 * pr + 3))
-    ship([1], "xn", lambda i: 16 * (pr % 2), "xr", "xn")
-    for h in (1, 2):
-        pair(batch[h][0][0])
-        ship(batch[h][0], "xd", lambda i: CAPP * who(i), "xr", "xa%d" % h)
+    pair(2, "xa0")
+    to_peer(near, "xl", V("off", 3 * who(1), 3 * who(1) + 3), V("poff", 0, 3), ap)
+    pair(4, "xa1")
+    pair(6, "xa2")
     if rank % 2:
         copy(V("ooff", 0, 3), V("off", 3 * rank, 3 * rank + 3))
     picks("xr", Z0, V("ooff", 0, 3) if rank % 2 else V("off", 3 * rank, 3 * rank + 3))
-
-    up, at = steps(1)
-    iota(V("tab", END - Z0, END + Z0 - 1), [[0, 2 * Z0 - 1]], -100)
-    for b in (0, 1):
-        c = END - 1 + Z0 + 4 * CAPP * b
-        iota(V("tab", c, c + 4 * CAPP), up[1:] + [[0, CAPP]], at + b * up[0][0])
-        c = 4 * CAPP * b
-        iota(V("tab", c, c + 4 * CAPP), up[1:] + [[0, CAPP]], -1 - who(7) + b * up[0][0])
+    up, at = steps(CAPP)
+    for k in range(4):
+        iota(V("ci", 128 + 8 * k, 136 + 8 * k), up, Z0 - 1 + at)
+    iota(V("bx", 0, 128), [[0, 4], [1, 2], [0, 16]], 0)
+    iota(V("bx", 128, FW), [[0, 16]], 0)
 
     for a in range(4):
         turn(V("fr", 32 + 32 * a, 64 + 32 * a), V("tr", 0, 32, 32 * a, 32 * a + 32))
     quant("wq", "wt")
-    turn(V("cc", 128, 224), V("ci", 128, 224))
     for a in range(4):
-        copy(V("rk", 0, TW, 32 * a, 32 * a + 32), V("fr", 32, 192), "v" if a > 1 else "s")
+        copy(V("rk", 0, FW, 32 * a, 32 * a + 32), V("fr", 32, 32 + FW), "v" if a > 1 else "s")
     for a in range(4):
-        copy(V("rk", 0, TW, 32 * a, 32 * a + 16), V("fr", 16, 176, 0, 16), "v" if a > 1 else "s")
-    act(V("pm"), V("bx"), ACT.Abs, bias=gcol)
-    memset(V("ones"), 1.0)
-    ts(V("nm"), V("rk"), 1.0, OP.is_le)
+        copy(V("rk", 0, FW, 32 * a, 32 * a + 16), V("fr", 16, 16 + FW, 0, 16), "v" if a > 1 else "s")
+    arrive("xf", 2 * len(every), [V("xf"), V("xfs")])
+    arrive("xl", len(near), [V("poff", 0, 3)])
+    picks("xr", Z0 + CAPP, V("poff", 0, 3), "xf")
     for t in range(4):
-        ts(V("ur", t, 512, st=4), V("ones"), V("ut", t, t + 1), OP.mult)
-    scan(V("ct"), V("nm"), V("zw"), 0.0)
+        fill(V("ur", t, 512, st=4), V("ut", t, t + 1))
+    ts(V("nm"), V("rk", 0, FW), 1.0, OP.is_le)
+    scan(V("ct"), V("nm"), V("zw", 0, FW), 0.0)
     quant("uq", "ur")
-    act(V("p1"), V("ct"), ACT.Identity, bias=pcol)
     act(V("ov"), V("ct"), ACT.Relu, scale=2.0, bias=-2.0 * CAPP)
-    ts(V("soff", 0, 1), lcol, 0.0, OP.max, 255.0, OP.min)
-    ts(V("soff", 1, 2), lcol, 128.0, OP.add, 255.0, OP.min)
 
-    land([1], "xr", "xn")
     for h, (places, c0, c1, w0, w1) in enumerate(batch):
         land([i for i in places if i > 1], "xr", "xa%d" % h)
         banks = [4 * (h % 2) + i for i in range(4)]
@@ -376,15 +374,26 @@ def rank_program(g, core, T, topo):
         quant("hq%d" % h, "ht", w0, w1)
         ship(places, "hq%d" % h, lambda i: Z0 + CAPP * i - w0, "hr", "ha%d" % h)
         if h == 0:
-            quant("hr", "ht", 0, LEAST)
-            tt(V("role"), V("rk"), V("ov"), OP.add)
+            turn(V("cc", 128, 160), V("ci", 128, 160))
         elif h == 1:
-            tt(V("p2"), V("p1"), V("pm"), OP.mult)
+            act(V("pm"), V("bx"), ACT.Abs, bias=gcol)
+            act(V("p1"), V("ct"), ACT.Identity, bias=pcol)
 
+    up, at = steps(1)
+    iota(V("tab", END - Z0, END + Z0 - 1), [[0, 2 * Z0 - 1]], -100)
+    for b in (0, 1):
+        c = END - 1 + Z0 + 4 * CAPP * b
+        iota(V("tab", c, c + 4 * CAPP), up[1:] + [[0, CAPP]], at + b * up[0][0])
+        c = 4 * CAPP * b
+        iota(V("tab", c, c + 4 * CAPP), up[1:] + [[0, CAPP]], -1 - who(7) + b * up[0][0])
+
+    tt(V("role"), V("rk", 0, FW), V("ov"), OP.add)
+    tt(V("p2"), V("p1"), V("pm"), OP.mult)
+    act(V("ma"), V("role"), ACT.Relu, scale=-1.0, bias=1.0)
     ts(V("mb"), V("role"), 1.0, OP.is_equal)
-    ts(V("ma"), V("role"), 0.0, OP.is_equal)
-    tt(V("vb"), V("mb"), V("p2"), OP.mult)
-    tt(V("va"), V("ma"), V("p2"), OP.mult)
+    quant("hr", "ht", 0, LEAST)
+    tt(V("vb", 0, FW), V("mb"), V("p2"), OP.mult)
+    tt(V("va", 0, FW), V("ma"), V("p2"), OP.mult)
     turn(V("tb"), V("vb"))
     turn(V("ta"), V("va"))
     runs(V("lab", 128, 256), V("seg"), V("tb", 8, 136))
@@ -397,12 +406,12 @@ def rank_program(g, core, T, topo):
     for h, (places, c0, c1, w0, w1) in enumerate(batch):
         land(places, "hr", "ha%d" % h)
         mm(h, "uq", 0, "hr", w0, w1)
-        mm(4 + h, "vq", 0, "hr", w0, w1)
         copy(V("qw", c0, c1), V("ps", BANK * h + c0 - w0, BANK * h + c1 - w0), "v" if h == last else "s")
-        if h == last:
-            for a, b in cuts:
-                copy(V("ga", a, b), V("qw"), "v", V("loff", a // 16, b // 16))
-                copy(V("gb", a, b), V("qw"), "s", V("loff", 16 + a // 16, 16 + b // 16))
+    for a, b in cuts:
+        copy(V("ga", a, b), V("qw"), "v", V("loff", a // 16, b // 16))
+        copy(V("gb", a, b), V("qw"), "s", V("loff", 16 + a // 16, 16 + b // 16))
+    for h, (places, c0, c1, w0, w1) in enumerate(batch):
+        mm(4 + h, "vq", 0, "hr", w0, w1)
         copy(V("yw", c0, c1), V("ps", BANK * (4 + h) + c0 - w0, BANK * (4 + h) + c1 - w0), "s")
     for a, b in cuts:
         tt(V("dd", a, b), V("gb", a, b), V("ga", a, b), OP.is_gt)
@@ -427,7 +436,8 @@ def rank_program(g, core, T, topo):
     dma("y", "dy", T.y[:, :], ap(V("ysb")), [], [V("ysb")])
     copy(V("zqs"), V("hrs"), "v", V("zoff"))
     act(V("wnr"), V("tab", 0, 2 * END - 1), ACT.Copy, V("toff"))
-    for k in range(4):
-        dma("s" if k < 2 else "y", "dos%d" % k, T.osc[4 * k:4 * k + 4, :], ap(V("zqs", 0, 128, 32 * k, 32 * k + 4)), [], [V("zqs")])
+    for k in range(3):
+        dma("y", "dos%d" % k, T.osc[4 * k:4 * k + 4, :], ap(V("zqs", 0, 128, 32 * k, 32 * k + 4)), [], [V("zqs")])
     dma("s", "dwn", T.wn[:, :], ap(V("wnr", 0, 128, 0, 1)), [], [V("wnr", 0, 128, 0, 1)])
+    dma("s", "dos3", T.osc[12:16, :], ap(V("zqs", 0, 128, 96, 100)), [], [V("zqs")])
     finish()

from concourse.bass import DstId, RemoteDMATransfer
from concourse.mybir import dt, AluOpType, AxisListType, ActivationFunctionType

OP, ACT = AluOpType, ActivationFunctionType
CAPP, CAPR = 48, 32
LEAST = 128
Z0 = LEAST - CAPP
END = Z0 + 8 * CAPP
FW = 144
CUT = 96
TW = 160
BIG = 9e29
BANK = 512

SCRATCH = {"ps": ("psum", [128, 8 * BANK], "float32"), "f0": ("sbuf", [32, 128], "bfloat16"),
           "zb": ("sbuf", [32, 128], "bfloat16"), "n4": ("sbuf", [128, 32], "bfloat16"),
           "lt": ("sbuf", [32, 32], "float32"), "fr": ("sbuf", [32, 192], "bfloat16"),
           "off": ("sbuf", [128, 24], "uint16"), "ooff": ("sbuf", [128, 4], "uint16"), "poff": ("sbuf", [128, 4], "uint16"),
           "loff": ("sbuf", [128, 32], "uint16"), "zoff": ("sbuf", [128, 8], "uint16"), "toff": ("sbuf", [128, 8], "uint16"),
           "aboff": ("sbuf", [128, 8], "uint16"), "soff": ("sbuf", [128, 2], "uint16")}
for _n, _w in (("xt", 512), ("zt", 512), ("rtt", 512), ("wt", 2048), ("ut", 512), ("ur", 512), ("vt", 512),
               ("ht", 4 * END), ("cb", 128), ("tmp", 256), ("tms", 256), ("zw", TW), ("r8", 8), ("tr", 32), ("rk", TW),
               ("nm", FW), ("ct", FW), ("ov", FW), ("role", FW), ("ma", FW), ("mb", FW), ("dd", FW), ("win", FW), ("cw", FW),
               ("hf", FW)):
    SCRATCH[_n] = ("sbuf", [128, _w], "bfloat16")
for _n, _w in (("xq", 2 * LEAST), ("rq", 128), ("rp", 128), ("wq", 512), ("uq", 128), ("vq", 128), ("xd", 384),
               ("xf", LEAST + 2), ("xr", END), ("hq0", 192), ("hq1", 128), ("hq2", 128), ("hr", END), ("zq", 128)):
    SCRATCH[_n] = ("sbuf", [128, _w], "float8_e4m3fn_x4")
    SCRATCH[_n + "s"] = ("sbuf", [128, _w], "uint8")
for _n, _w in (("ci", 224), ("cc", 224), ("c2", 4), ("bc", 1), ("sc", 1), ("bx", FW), ("pm", FW), ("zero", TW), ("d0", 64),
               ("thr", 8), ("c8", 8), ("seg", 128), ("bs", 64), ("cp", 64), ("sg", 64), ("lc", 4), ("of", 32),
               ("p1", FW), ("p2", FW), ("va", TW), ("vb", TW), ("ta", TW), ("tb", TW), ("lab", 256), ("tab", 2 * END),
               ("qw", END), ("yw", END), ("ga", FW), ("gb", FW), ("xp", FW), ("val", TW), ("tv", TW), ("s8", 128),
               ("wnr", 128), ("ysb", 128)):
    SCRATCH[_n] = ("sbuf", [128, _w], "float32")
DMAS = ["dx", "drt", "dw0", "dw1", "du", "dv", "doc", "dos0", "dos1", "dos2", "dos3", "dy", "dwn"]
SEMAPHORES = ["cv", "cs", "ct", "cg", "ls", "xf", "xl", "xa0", "xa1", "xa2", "ha0", "ha1", "ha2"] + DMAS


def _runner(g, T):
    queues = {"v": g.vector, "s": g.scalar, "t": g.tensor, "g": g, "y": g.sync}
    own = {"v": "cv", "s": "cs", "t": "ct", "g": "cg"}
    total, known, snap, recs = {}, {q: {} for q in queues}, {}, {}

    def region(view):
        b, p0, p1, c0, c1, st = view
        if SCRATCH[b][0] == "psum":
            return (0, 128, c0 // BANK * BANK, -(-c1 // BANK) * BANK, 1)
        return (p0, p1, c0, c1, st)

    def meet(a, b):
        if a[0] >= b[1] or b[0] >= a[1] or a[2] >= b[3] or b[2] >= a[3]:
            return False
        return not (a[4] > 1 and a[4] == b[4] and (a[2] - b[2]) % a[4])

    def wait_for(q, need):
        need = [(s, v) for s, v in need.items() if known[q].get(s, 0) < v]
        for i, (s, v) in enumerate(need):
            if any(snap.get(o, {}).get(s, 0) >= v for j, o in enumerate(need) if j != i):
                continue
            queues[q].wait_ge(T.sem[s], v)
        for s, v in need:
            known[q][s] = max(known[q].get(s, 0), v)
            for s2, v2 in snap.get((s, v), {}).items():
                known[q][s2] = max(known[q].get(s2, 0), v2)

    def wants(q, outs, ins):
        need = {}
        for wr, views in ((True, outs), (False, ins)):
            for view in views:
                r = region(view)
                ps = SCRATCH[view[0]][0] == "psum"
                for w, r2, tok, q2 in recs.get(view[0], []):
                    if not (wr or w or (ps and q2 != q)) or not meet(r, r2):
                        continue
                    need[tok[0]] = max(need.get(tok[0], 0), tok[1])
        return need

    def note(q, outs, ins, tok):
        for wr, views in ((True, outs), (False, ins)):
            for view in views:
                recs.setdefault(view[0], []).append((wr, region(view), tok, q))

    def op(q, call, outs, ins, dma=None):
        wait_for(q, wants(q, outs, ins))
        sem, n = (dma, 16) if dma else (own[q], 1)
        call(queues[q]).then_inc(T.sem[sem], n)
        total[sem] = total.get(sem, 0) + n
        tok = (sem, total[sem])
        snap[tok] = dict(known[q])
        note(q, outs, ins, tok)

    def arrive(sem, n, outs):
        total[sem] = total.get(sem, 0) + n
        note("far", outs, [], (sem, total[sem]))

    def send(call, ins, ls):
        wait_for("g", wants("g", [], ins))
        call(g)
        total["ls"] = total.get("ls", 0) + ls

    def finish():
        wait_for("g", dict(total))

    return op, arrive, send, finish


def rank_program(g, core, T, topo):
    rank = T.rank_of(core)
    if rank is None:
        return
    op, arrive, send, finish = _runner(g, T)
    N = len(T.cores)

    def who(i):
        return rank ^ i

    batch = []
    for p0, n in ((0, 4), (4, 2), (6, 2)):
        c0, c1 = Z0 + CAPP * p0, Z0 + CAPP * (p0 + n)
        batch.append((list(range(p0, p0 + n)), c0, c1, min(c0, c1 - LEAST), c1))
    chip = [topo.chip(c) for c in T.cores]
    away = topo.engines(core, next(c for c in T.cores if topo.chip(c) != topo.chip(core)))
    peer = next(c for c in T.cores if topo.chip(c) == topo.chip(core) and c != core)
    every = topo.engines(core, peer)
    near = [e for e in every if e not in away][:len(away) // 2]

    def bits(es):
        return sum(1 << e for e in es)

    def V(b, c0=0, c1=None, p0=0, p1=None, st=1):
        sh = SCRATCH[b][1]
        return (b, p0, sh[0] if p1 is None else p1, c0, sh[1] if c1 is None else c1, st)

    def ap(v):
        b, p0, p1, c0, c1, st = v
        return T[b][p0:p1, c0:c1] if st == 1 else T[b][p0:p1, c0:c1:st]

    def by(v):
        return ap(v).bitcast(dt.uint8)

    def memset(v, x):
        op("v", lambda q: q.memset(ap(v), x), [v], [])

    def act(out, in_, f, lst=None, acc=None, **k):
        src = ap(in_) if lst is None else ap(in_).indirect(ap(lst))
        cols = [x for x in k.values() if isinstance(x, tuple)]
        kk = {n: ap(x) if isinstance(x, tuple) else x for n, x in k.items()}
        if acc is not None:
            kk["accum_out"] = ap(acc)
        op("s", lambda q: q.activation(ap(out), src, f, **kk), [out] + ([acc] if acc else []),
           [in_] + cols + ([lst] if lst else []))

    def fill(v, x):
        n = len(range(v[3], v[4], v[5]))
        act(v, V("zero", 0, n, v[1], v[2]), ACT.Identity, bias=x)

    def copy(out, in_, q="v", lst=None):
        if q == "v":
            src = ap(in_) if lst is None else ap(in_).indirect(ap(lst))
            op("v", lambda e: e.tensor_copy(ap(out), src), [out], [in_] + ([lst] if lst else []))
        else:
            act(out, in_, ACT.Copy, lst)

    def tt(out, a, b, o):
        op("v", lambda q: q.tensor_tensor(ap(out), ap(a), ap(b), o), [out], [a, b])

    def ts(out, a, s1, o1, s2=None, o2=None):
        ins = [a] + [s for s in (s1, s2) if isinstance(s, tuple)]
        x1, x2 = (ap(s) if isinstance(s, tuple) else s for s in (s1, s2))
        if o2 is None:
            op("v", lambda q: q.tensor_scalar(ap(out), ap(a), x1, None, o1), [out], ins)
        else:
            op("v", lambda q: q.tensor_scalar(ap(out), ap(a), x1, x2, o1, o2), [out], ins)

    def total(out, in_):
        op("v", lambda e: e.tensor_reduce(ap(out), ap(in_), AxisListType.X, OP.add), [out], [in_])

    def runs(out, mask, in_):
        op("v", lambda q: q.tensor_tensor_scan(ap(out), ap(mask), ap(in_), 0.0, OP.mult, OP.add), [out], [mask, in_])

    def scan(out, a, b, init):
        ini = ap(init) if isinstance(init, tuple) else init
        op("v", lambda q: q.tensor_tensor_scan(ap(out), ap(a), ap(b), ini, OP.add, OP.add), [out],
           [a, b] + ([init] if isinstance(init, tuple) else []))

    def turn(out, in_):
        op("v", lambda q: q.transpose(ap(out), ap(in_)), [out], [in_])

    def quant(c, t, a=0, b=None, d=0):
        n = SCRATCH[t][1][1] // 4 if b is None else b - a
        o, s, i = V(c, d, d + n), V(c + "s", d, d + n), V(t, 4 * a, 4 * (a + n))
        op("v", lambda q: q.quantize_mx(ap(o), ap(s), ap(i)), [o, s], [i])

    def mm(bank, l, la, r, ra, rb):
        out, lc, ls, rc, rs = V("ps", BANK * bank, BANK * bank + rb - ra), V(l, la, la + 128), V(l + "s", la, la + 128), V(r, ra, rb), V(r + "s", ra, rb)
        op("t", lambda q: q.matmul_mx(ap(out), ap(lc), ap(ls), ap(rc), ap(rs), True, True), [out], [lc, ls, rc, rs])

    def pick(o, w, lst):
        op("v", lambda q: q.tensor_copy(ap(o).bitcast(dt.uint32), ap(w).bitcast(dt.uint32).indirect(ap(lst))), [o], [w, lst])

    def picks(dst, d, lst, src="xq"):
        n = 16 * (lst[4] - lst[3])
        pick(V(dst, d, d + n), V(src), lst)
        act(V(dst + "s", d, d + n), V(src + "s"), ACT.Copy, lst)

    def dma(q, sem, dst, src, outs, ins):
        op(q, lambda e: e.dma_start(dst, src), outs, ins, dma=sem)

    def transfer(to, eng, sem, src, dst):
        rid, pid, _s = topo.addr(to)
        return RemoteDMATransfer(dst_ids=[DstId(rid=rid, pnc=pid)], dma_engine_mask=bits(eng), remote_sem=T.sem[sem], src=src, dst=dst)

    def to_peer(eng, sem, s, d, f):
        send(lambda q: q.remote_dma_fused([transfer(peer, eng, sem, f(s), f(d))], local_sem=T.sem["ls"]), [s], len(eng))

    def parts(places):
        to = [i for i in places if i > 0]
        far = [i for i in to if chip[who(i)] != topo.chip(core)]
        return to, far, len(away) // max(len(far), 1)

    def ship(places, src, s0, dst, sem):
        to, far, k = parts(places)
        for x, f in (("", by), ("s", ap)):
            trs, ins, ls = [], [], 0
            for i in to:
                eng = near if i not in far else away[k * far.index(i):k * far.index(i) + k]
                a, d0 = s0(i), Z0 + CAPP * i
                s, d = V(src + x, a, a + CAPP), V(dst + x, d0, d0 + CAPP)
                trs.append(transfer(T.cores[who(i)], eng, sem, f(s), f(d)))
                ins.append(s)
                ls += len(eng)
            send(lambda q: q.remote_dma_fused(trs, local_sem=T.sem["ls"]), ins, ls)

    def land(places, dst, sem):
        to, far, k = parts(places)
        n = 2 * (len(far) * k + len(near) * (len(to) - len(far)))
        arrive(sem, n, [V(dst + x, Z0 + CAPP * i, Z0 + CAPP * i + CAPP) for i in to for x in ("", "s")])

    dma("s", "drt", ap(V("rtt", 0, 4 * N)), T.rt[:, 0:4 * N], [V("rtt", 0, 4 * N)], [])
    dma("y", "dx", ap(V("xt")), T.x[:, :], [V("xt")], [])
    dma("y", "dv", ap(V("vt")), T.v[:, :], [V("vt")], [])
    dma("y", "dw0", ap(V("wt", 0, 1024)), T.w[:, 0:1024], [V("wt", 0, 1024)], [])
    dma("y", "dw1", ap(V("wt", 1024, 2048)), T.w[:, 1024:2048], [V("wt", 1024, 2048)], [])
    dma("y", "du", ap(V("ut")), T.u[:, :], [V("ut")], [])

    def iota(v, pattern, b, cm=0):
        op("g", lambda q: q.iota(ap(v), pattern, b, cm, allow_small_or_imprecise_dtypes=True), [v], [])

    def steps(w):
        return [[-w * b if rank & b else w * b, 2] for b in (4, 2, 1)], w * rank

    iota(V("ci", 0, 32), [[0, 4], [1, 8]], 0)
    iota(V("ci", 32, 64), [[0, 2], [1, 2], [0, 8]], 0)
    iota(V("c2"), [[2, 4]], 0)
    iota(V("ci", 64, 88), [[0, 8], [-16, 3]], 0, -4)
    iota(V("ci", 88, 96), [[0, 8]], 0)
    iota(V("ci", 96, 128), [[0, 8], [1, 4]], 0)
    iota(V("thr"), [[-1, 8]], 7)
    iota(V("c8"), [[-1, 8]], 8)
    iota(V("ci", 160, 192), [[0, 2], [1, 2], [0, 8]], -1)
    iota(V("ci", 192, 224), [[16, 2], [16, 16]], -1)
    ecol, hcol, mcol, pcol, gcol, lcol = (V("cc", c, c + 1) for c in (0, 32, 96, 128, 160, 192))
    memset(V("zero"), 0.0)
    memset(V("rtt", 4 * N, 512), 0.0)
    memset(V("d0"), 1.0)
    memset(V("d0", 9, 64, st=9), -1.0)
    memset(V("d0", 0, 64, st=8), 0.0)
    turn(V("cc", 0, 64), V("ci", 0, 64))
    ts(V("aboff", 0, 4), V("c2"), hcol, OP.add, ecol, OP.min)
    ts(V("aboff", 4, 8), V("c2"), hcol, OP.add, ecol, OP.max)
    for c in range(0, 512, TW):
        fill(V("zt", c, min(c + TW, 512)), 0.0)
    fill(V("n4", 24, 32), 0.0)
    fill(V("zb"), 0.0)

    quant("rq", "rtt")
    pick(V("rp"), V("rq"), V("aboff"))
    act(V("rps"), V("rqs"), ACT.Copy, V("aboff"))
    quant("xq", "xt", 0, LEAST)
    mm(0, "xq", 0, "rp", 0, 128)
    quant("xq", "zt", 0, LEAST, LEAST)
    to_peer(every, "xf", V("xq", 0, LEAST + 2), V("xf"), by)
    to_peer(every, "xf", V("xqs", 0, LEAST + 2), V("xfs"), ap)
    copy(V("bs"), V("ps", 64, 128))
    turn(V("cc", 64, 128), V("ci", 64, 128))
    tt(V("cp"), V("ps", 0, 64), V("bs"), OP.is_ge)
    runs(V("sg"), V("d0"), V("cp"))
    ts(V("bc"), mcol, 1.5, OP.is_ge, 64.0, OP.mult)
    rank8 = V("sg", 7, 64, st=8)
    for k in range(3):
        tt(V("n4", k, 24, st=3), rank8, V("thr"), OP.is_ge)
    tt(V("r8"), V("c8"), rank8, OP.subtract)
    for c0 in (0, 160):
        fill(V("fr", c0, c0 + 32), 8.0)
    fill(V("zw"), 0.0)
    for c in range(0, 4 * Z0, TW):
        fill(V("ht", c, c + TW), 0.0)
    for b in ("val", "va", "vb"):
        fill(V(b, FW, TW), 0.0)
    fill(V("seg"), 1.0)
    fill(V("qw", 0, Z0), -BIG)
    fill(V("yw", 0, Z0), 0.0)
    fill(V("seg", 0, 128, st=16), 0.0)
    for a in range(4):
        turn(V("f0", 32 * a, 32 * a + 32), V("n4", 0, 32, 32 * a, 32 * a + 32))
    ts(V("sc"), V("bc"), -1.0 / 128, OP.mult, 1.0, OP.add)
    for a in range(4):
        scan(V("cb", 0, 128, 32 * a, 32 * a + 32), V("f0"), V("zb"), V("cc", 64 + a, 65 + a, 0, 32))
    for j in range(4):
        copy(V("tr", 8 * j, 8 * j + 8), V("r8"), "s")
    for m in (2, 3):
        act(V("tms", 128 * m - 256, 128 * m - 128), V("cb"), ACT.Sign, acc=V("lc", m, m + 1), bias=m + 0.5, scale=-1.0)
    turn(V("cc", 160, 224), V("ci", 160, 224))
    for m in (0, 1):
        ts(V("tmp", 128 * m, 128 * m + 128), V("cb"), float(m), OP.is_le)
    for m in (0, 1):
        total(V("lc", m, m + 1), V("tmp", 128 * m, 128 * m + 128))
    ts(V("soff", 0, 1), lcol, 0.0, OP.max, 255.0, OP.min)
    for a in range(4):
        for d in (0, 16):
            copy(V("lt", d + 4 * a, d + 4 * a + 4), V("lc", 0, 4, 32 * a, 32 * a + 32), "s" if d else "v")
    ts(V("soff", 1, 2), lcol, 128.0, OP.add, 255.0, OP.min)
    for a in range(4):
        turn(V("of", 0, 32, 32 * a, 32 * a + 32), V("lt"))
    ts(V("off"), V("of", 0, 24), V("sc"), OP.mult, V("bc"), OP.add)

    def pair(i, sem):
        e = who(i) // 2 * 2
        picks("xd", CAPP * e, V("off", 3 * e, 3 * e + 6))
        ship([i, i + 1], "xd", lambda j: CAPP * who(j), "xr", sem)

    pair(2, "xa0")
    to_peer(near, "xl", V("off", 3 * who(1), 3 * who(1) + 3), V("poff", 0, 3), ap)
    pair(4, "xa1")
    pair(6, "xa2")
    if rank % 2:
        copy(V("ooff", 0, 3), V("off", 3 * rank, 3 * rank + 3))
    picks("xr", Z0, V("ooff", 0, 3) if rank % 2 else V("off", 3 * rank, 3 * rank + 3))
    up, at = steps(CAPP)
    for k in range(4):
        iota(V("ci", 128 + 8 * k, 136 + 8 * k), up, Z0 - 1 + at)
    iota(V("bx", 0, 128), [[0, 4], [1, 2], [0, 16]], 0)
    iota(V("bx", 128, FW), [[0, 16]], 0)

    for a in range(4):
        turn(V("fr", 32 + 32 * a, 64 + 32 * a), V("tr", 0, 32, 32 * a, 32 * a + 32))
    quant("wq", "wt")
    for a in range(4):
        copy(V("rk", 0, FW, 32 * a, 32 * a + 32), V("fr", 32, 32 + FW), "v" if a > 1 else "s")
    for a in range(4):
        copy(V("rk", 0, FW, 32 * a, 32 * a + 16), V("fr", 16, 16 + FW, 0, 16), "v" if a > 1 else "s")
    arrive("xf", 2 * len(every), [V("xf"), V("xfs")])
    arrive("xl", len(near), [V("poff", 0, 3)])
    picks("xr", Z0 + CAPP, V("poff", 0, 3), "xf")
    for t in range(4):
        fill(V("ur", t, 512, st=4), V("ut", t, t + 1))
    ts(V("nm"), V("rk", 0, FW), 1.0, OP.is_le)
    scan(V("ct"), V("nm"), V("zw", 0, FW), 0.0)
    quant("uq", "ur")
    act(V("ov"), V("ct"), ACT.Relu, scale=2.0, bias=-2.0 * CAPP)

    for h, (places, c0, c1, w0, w1) in enumerate(batch):
        land([i for i in places if i > 1], "xr", "xa%d" % h)
        banks = [4 * (h % 2) + i for i in range(4)]
        for i in (0, 2, 1, 3):
            mm(banks[i], "wq", 128 * i, "xr", w0, w1)
        for i in range(4):
            r, o = V("ps", BANK * banks[i] + c0 - w0, BANK * banks[i] + c1 - w0), V("ht", 4 * c0 + i, 4 * c1, st=4)
            if i < 2:
                ts(o, r, 0.0, OP.max, 0.0625, OP.mult)
            else:
                act(o, r, ACT.Relu, scale=0.0625)
        quant("hq%d" % h, "ht", w0, w1)
        ship(places, "hq%d" % h, lambda i: Z0 + CAPP * i - w0, "hr", "ha%d" % h)
        if h == 0:
            turn(V("cc", 128, 160), V("ci", 128, 160))
        elif h == 1:
            act(V("pm"), V("bx"), ACT.Abs, bias=gcol)
            act(V("p1"), V("ct"), ACT.Identity, bias=pcol)

    up, at = steps(1)
    iota(V("tab", END - Z0, END + Z0 - 1), [[0, 2 * Z0 - 1]], -100)
    for b in (0, 1):
        c = END - 1 + Z0 + 4 * CAPP * b
        iota(V("tab", c, c + 4 * CAPP), up[1:] + [[0, CAPP]], at + b * up[0][0])
        c = 4 * CAPP * b
        iota(V("tab", c, c + 4 * CAPP), up[1:] + [[0, CAPP]], -1 - who(7) + b * up[0][0])

    tt(V("role"), V("rk", 0, FW), V("ov"), OP.add)
    tt(V("p2"), V("p1"), V("pm"), OP.mult)
    act(V("ma"), V("role"), ACT.Relu, scale=-1.0, bias=1.0)
    ts(V("mb"), V("role"), 1.0, OP.is_equal)
    quant("hr", "ht", 0, LEAST)
    tt(V("vb", 0, FW), V("mb"), V("p2"), OP.mult)
    tt(V("va", 0, FW), V("ma"), V("p2"), OP.mult)
    turn(V("tb"), V("vb"))
    turn(V("ta"), V("va"))
    runs(V("lab", 128, 256), V("seg"), V("tb", 8, 136))
    runs(V("lab", 0, 128), V("seg"), V("ta", 8, 136))
    quant("vq", "vt")
    copy(V("loff"), V("lab"), "v", V("soff"))

    last = len(batch) - 1
    cuts = ((0, CUT), (CUT, FW))
    for h, (places, c0, c1, w0, w1) in enumerate(batch):
        land(places, "hr", "ha%d" % h)
        mm(h, "uq", 0, "hr", w0, w1)
        copy(V("qw", c0, c1), V("ps", BANK * h + c0 - w0, BANK * h + c1 - w0), "v" if h == last else "s")
    for a, b in cuts:
        copy(V("ga", a, b), V("qw"), "v", V("loff", a // 16, b // 16))
        copy(V("gb", a, b), V("qw"), "s", V("loff", 16 + a // 16, 16 + b // 16))
    for h, (places, c0, c1, w0, w1) in enumerate(batch):
        mm(4 + h, "vq", 0, "hr", w0, w1)
        copy(V("yw", c0, c1), V("ps", BANK * (4 + h) + c0 - w0, BANK * (4 + h) + c1 - w0), "s")
    for a, b in cuts:
        tt(V("dd", a, b), V("gb", a, b), V("ga", a, b), OP.is_gt)
    for a, b in cuts:
        tt(V("win", a, b), V("dd", a, b), V("role", a, b), OP.is_equal)
    for a, b in cuts:
        scan(V("cw", a, b), V("win", a, b), V("zw", a, b), V("cw", a - 1, a) if a else 0.0)
        act(V("hf", a, b), V("cw", a, b), ACT.Sign, bias=CAPR + 0.5, scale=-1.0)
        tt(V("xp", a, b), V("win", a, b), V("p2", a, b), OP.mult)
    for a, b in cuts:
        tt(V("val", a, b), V("xp", a, b), V("hf", a, b), OP.mult)
    turn(V("tv", 0, CUT), V("val", 0, CUT))
    turn(V("tv", CUT, TW), V("val", CUT, TW))
    for a, b in ((0, CUT - 16), (CUT - 16, 128)):
        runs(V("s8", a, b), V("seg", a, b), V("tv", 8 + a, 8 + b))
    s = V("s8", 15, 128, st=16)
    copy(V("zoff"), s)
    ts(V("toff"), s, float(END - 1), OP.add)
    pick(V("zq"), V("hr"), V("zoff"))
    dma("y", "doc", T.oc[:, :], by(V("zq")), [], [V("zq")])
    act(V("ysb"), V("yw"), ACT.Copy, V("zoff"))
    dma("y", "dy", T.y[:, :], ap(V("ysb")), [], [V("ysb")])
    copy(V("zqs"), V("hrs"), "v", V("zoff"))
    act(V("wnr"), V("tab", 0, 2 * END - 1), ACT.Copy, V("toff"))
    for k in range(3):
        dma("y", "dos%d" % k, T.osc[4 * k:4 * k + 4, :], ap(V("zqs", 0, 128, 32 * k, 32 * k + 4)), [], [V("zqs")])
    dma("s", "dwn", T.wn[:, :], ap(V("wnr", 0, 128, 0, 1)), [], [V("wnr", 0, 128, 0, 1)])
    dma("s", "dos3", T.osc[12:16, :], ap(V("zqs", 0, 128, 96, 100)), [], [V("zqs")])
    finish()
